import numpy as np
import ml_dtypes


def mxq(x, axis, fmt="e4m3"):
    dtype, down = {"e4m3": (ml_dtypes.float8_e4m3fn, 7), "e5m2": (ml_dtypes.float8_e5m2, 14)}[fmt]
    v = np.moveaxis(np.asarray(x, np.float32).astype(ml_dtypes.bfloat16).astype(np.float64), axis, -1)
    blocks = v.reshape(v.shape[:-1] + (-1, 32))
    amax = np.abs(blocks).max(-1, keepdims=True)
    byte = np.maximum(np.where(amax > 0, np.frexp(amax)[1] - 1 + 127, 0) - down, 1)
    scale = np.exp2(byte - 127.0)
    codes = (blocks / scale).astype(np.float32).astype(dtype).astype(np.float64)
    return np.moveaxis((codes * scale).reshape(v.shape), -1, axis)


WIDE = False


def mx_kscale(k):
    if not WIDE:
        return np.ones(k)
    levels = np.array([10, -10, 5, -5, 0])
    if k % 512:
        return np.exp2(np.random.permutation(np.resize(levels, k // 32))).repeat(32)
    a = np.empty((k // 512, 16))
    for p in range(k // 512):
        a[p, :8] = np.random.permutation(np.resize(levels, 8))
        for g in range(8):
            far = levels[np.abs(levels - a[p, g]) >= 10]
            a[p, g + 8] = far[np.random.randint(len(far))]
    return np.exp2(a.ravel()).repeat(32)


def f64(x):
    return np.asarray(x).astype(np.float64)


def striped(idx):
    return np.tile(idx.reshape(-1, 16).T, (8, 1)).astype(np.uint16)


def unstriped(offs):
    return offs[:16].T.reshape(-1).astype(np.int64)


def striped8(idx):
    return np.concatenate([x.reshape(-1, 16).T for x in idx]).astype(np.uint16)


def runs(offs, k):
    lists = np.stack([offs[16 * r : 16 * r + 16].T.reshape(-1) for r in range(8)]).astype(np.int64)
    return lists[np.arange(k) % 512 // 64]


def pack_weight(w):
    k, n = w.shape
    w = f64(np.asarray(w, np.float32).astype(ml_dtypes.bfloat16)).reshape(k // 32, 32, n)
    amax = np.abs(w).max(1)
    byte = np.clip(np.where(amax > 0, np.frexp(amax)[1] - 1 + 127 - 7, 1), 1, 254)
    scaled = (w * np.exp2(127.0 - byte)[:, None, :]).reshape(k, n).astype(np.float32)
    words = np.ascontiguousarray(scaled.reshape(k // 512, 128, 4, n).transpose(0, 1, 3, 2)).astype(ml_dtypes.float8_e4m3fn).view(np.uint8)
    return words, np.ascontiguousarray(byte.astype(np.uint8).reshape(k // 512, 16, n))


def unpack_weight(words, scales):
    g, p, n, _ = words.shape
    vals = np.ascontiguousarray(words).view(ml_dtypes.float8_e4m3fn).astype(np.float64) * np.repeat(np.exp2(scales.astype(np.float64) - 127.0), 8, axis=1)[..., None]
    return vals.transpose(0, 1, 3, 2).reshape(g * 512, n)


def relu(v):
    return np.maximum(v, 0.0)


K, T, S, N = 512, 2048, 512, 512


def setup_inputs():
    n = np.random.standard_normal
    s = mx_kscale(K)[:, None]
    packed_xT = pack_weight(n((K, T)) * s)
    return {
        "x_words": packed_xT[0],
        "x_scales": packed_xT[1],
        "w1": (n((K, N)) / np.sqrt(K) / s).astype(np.float32),
        "w2": (n((K, N)) / np.sqrt(K) / s).astype(np.float32),
        "tau": np.random.uniform(0.1, 0.9, (N, S)).astype(np.float32),
        "offs": striped8(np.stack([np.random.permutation(T)[:S] for _ in range(8)])),
        "obs": striped(np.random.permutation(T)[:S]),
        "at": striped8(np.stack([np.random.permutation(S) for _ in range(8)])),
    }


def reference(x_words, x_scales, w1, w2, tau, offs, obs, at):
    x_obs = unpack_weight(x_words, x_scales)[:, unstriped(obs)]
    e = mxq(f64(w2), 0, "e4m3").T @ x_obs
    xq = unpack_weight(x_words, x_scales)[np.arange(K)[:, None], runs(offs, K)]
    y = mxq(f64(w1), 0, "e4m3").T @ xq
    d = e[np.arange(N)[:, None], runs(at, N)] - y
    return f64(tau) * d - (d - relu(d))

@@ -1,0 +1,142 @@
+from contextlib import ExitStack
+
+import concourse.mybir as mybir
+
+K, T, S, N = 512, 2048, 512, 512
+FLOPS = 2 * 2 * K * N * S
+
+F32 = mybir.dt.float32
+BF16 = mybir.dt.bfloat16
+I32 = mybir.dt.int32
+U32 = mybir.dt.uint32
+U16 = mybir.dt.uint16
+U8 = mybir.dt.uint8
+FP8X4 = mybir.dt.float8_e4m3fn_x4
+ALU = mybir.AluOpType
+COPY = mybir.ActivationFunctionType.Copy
+
+P = 128
+PACK = 4
+QUAD = 32
+GROUP = 16
+HALF = S // 2
+M_VECTOR = 84
+
+
+def tile_picked_pinball_none_p_kernel(
+    tc, x_words, x_scales, w1, w2, tau, offs, obs, at, out
+):
+    nc = tc.nc
+    with ExitStack() as ctx:
+        keep = ctx.enter_context(tc.tile_pool(name="keep", bufs=1))
+        psum = ctx.enter_context(tc.psum_pool(name="psum", bufs=1))
+
+        offs_sb = keep.tile([P, S // GROUP], U16, name="offs_sb")
+        obs_sb = keep.tile([P, S // GROUP], U16, name="obs_sb")
+        at_sb = keep.tile([P, S // GROUP], U16, name="at_sb")
+        scale_table = keep.tile([P, T], U8, name="scale_table", align_bytes=64)
+        word_table = keep.tile([P, T], U32, name="word_table", align_bytes=64)
+        x_planes = keep.tile([P, 2 * S], U8, name="x_planes", align_bytes=64)
+
+        nc.gpsimd.memset(x_planes[:].bitcast(I32), 0)
+        nc.sync.dma_start(offs_sb[:], offs)
+        nc.sync.dma_start(obs_sb[:], obs)
+        rows = x_scales[0].bitcast(I32)
+        nc.sync.dma_start(scale_table[:].bitcast(I32), rows.unsqueeze(1).to_broadcast([16, 8, T // 4]))
+
+        raw = {}
+        raw["w2"] = keep.tile([P, PACK, N], F32, name="raw_w2", tag="w2_then_tau")
+        raw["w1"] = keep.tile([P, PACK, N], F32, name="raw_w1")
+        nc.sync.dma_start(raw["w2"][:], w2.rearrange("(p j) c -> p j c", j=PACK))
+        nc.sync.dma_start(word_table[:].bitcast(I32), x_words[0].rearrange("p c r -> p (c r)").bitcast(I32))
+        nc.sync.dma_start(raw["w1"][:], w1.rearrange("(p j) c -> p j c", j=PACK))
+        nc.sync.dma_start(at_sb[:], at)
+        tau_rows = tau.rearrange("(p t) s -> p t s", t=PACK)
+        out_rows = out.rearrange("(p t) s -> p t s", t=PACK)
+
+        picked_scales = keep.tile([P, 2 * S], U8, name="picked_scales", align_bytes=64)
+        e_words = keep.tile([P, S], U32, name="e_words", align_bytes=64)
+        y_words = keep.tile([P, S], U32, name="y_words", align_bytes=64)
+        nc.vector.tensor_copy(picked_scales[:, :S], scale_table[:].indirect(obs_sb[:]))
+        nc.vector.tensor_copy(picked_scales[:, S:], scale_table[:].indirect(offs_sb[:]))
+        for r in range(PACK):
+            nc.scalar.dma_start(x_planes[:].bitcast(I32)[r:P:QUAD, :], picked_scales[:].bitcast(I32)[8 * r : P : QUAD, :])
+        nc.vector.tensor_copy(e_words[:], word_table[:].indirect(obs_sb[:]))
+        nc.vector.tensor_copy(y_words[:], word_table[:].indirect(offs_sb[:]))
+
+        whole = slice(0, S)
+        halves = [slice(0, HALF), slice(HALF, S)]
+
+        def y_pieces(t):
+            return [("y0", halves[0]), ("e0", halves[1])] if t == 0 else [("y%d" % t, whole)]
+
+        def product(name, words, scales, sign, pieces):
+            grouped = keep.tile([P, PACK, P, PACK], BF16, name="grouped_" + name, align_bytes=64)
+            codes = keep.tile([P, N], U32, name="codes_" + name, align_bytes=64)
+            planes = keep.tile([P, N], U8, name="planes_" + name, align_bytes=64)
+            dst = grouped[:].rearrange("p t m j -> p m j t")
+            src = raw[name][:].rearrange("p j (m t) -> p m j t", t=PACK)
+            nc.vector.tensor_copy(dst[:, :M_VECTOR], src[:, :M_VECTOR])
+            nc.scalar.copy(dst[:, M_VECTOR:], src[:, M_VECTOR:])
+            results = []
+            for t in range(PACK):
+                cols = slice(P * t, P * (t + 1))
+                nc.vector.quantize_mx(
+                    out=codes[:, cols].bitcast(FP8X4),
+                    scales=planes[:, cols],
+                    in_=grouped[:, t].rearrange("p m j -> p (m j)"),
+                )
+            for t in range(PACK):
+                cols = slice(P * t, P * (t + 1))
+                result = keep.tile([P, S], F32, name="res_%s_%d" % (name, t))
+                for bank, places in pieces(t):
+                    acc = psum.tile([P, places.stop - places.start], F32, name="acc", tag=bank)
+                    nc.tensor.matmul_mx(
+                        out=acc[:],
+                        lhsT=codes[:, cols].bitcast(FP8X4),
+                        lhsT_scale=planes[:, cols],
+                        rhs=words[:, places].bitcast(FP8X4),
+                        rhs_scale=scales[:, places],
+                        start=True,
+                        stop=True,
+                    )
+                    nc.scalar.activation(result[:, places], acc[:], COPY, scale=sign)
+                results.append(result)
+            return results
+
+        neg_e = product("w2", e_words, x_planes[:, :S], -1.0, lambda t: [("e%d" % t, whole)])
+        tau_all = keep.tile([P, PACK, S], F32, name="tau_all", tag="w2_then_tau")
+        for u in range(2):
+            nc.sync.dma_start(tau_all[:, 2 * u : 2 * u + 2, :], tau_rows[:, 2 * u : 2 * u + 2, :])
+        tau_sb = [tau_all[:, t, :] for t in range(PACK)]
+        y = product("w1", y_words, x_planes[:, S:], 1.0, y_pieces)
+
+        miss = [keep.tile([P, S], F32, name="miss_%d" % t) for t in range(PACK)]
+        tilt = [keep.tile([P, S], F32, name="tilt_%d" % t) for t in range(PACK)]
+        loss = [keep.tile([P, S], F32, name="loss_%d" % t) for t in range(PACK)]
+
+        def gather(t, h):
+            cols = slice(HALF * h, HALF * (h + 1))
+            entries = at_sb[:, HALF // GROUP * h : HALF // GROUP * (h + 1)]
+            nc.vector.tensor_tensor(miss[t][:, cols], neg_e[t][:].indirect(entries), y[t][:, cols], ALU.add)
+
+        def weigh(t, cols):
+            nc.vector.tensor_tensor(tilt[t][:, cols], miss[t][:, cols], tau_sb[t][:, cols], ALU.mult)
+
+        def finish(t, cols):
+            nc.vector.scalar_tensor_tensor(
+                loss[t][:, cols], miss[t][:, cols], 0.0, tilt[t][:, cols], ALU.max, ALU.subtract
+            )
+            nc.sync.dma_start(out_rows[:, t, cols], loss[t][:, cols])
+
+        gather(0, 0)
+        gather(0, 1)
+        for t in range(1, PACK):
+            gather(t, 0)
+            weigh(t - 1, whole)
+            gather(t, 1)
+            finish(t - 1, whole)
+        for cols in halves:
+            weigh(PACK - 1, cols)
+        for cols in halves:
+            finish(PACK - 1, cols)

@@ -20,7 +20,10 @@ PACK = 4
 QUAD = 32
 GROUP = 16
 HALF = S // 2
-M_VECTOR = 84
+M_HALF = P // 2
+W2_VECTOR = (0, 44)
+W1_VECTOR = (64, 64)
+E_BANKS = ("e0", "e1", "e2", "e3")
 
 
 def tile_picked_pinball_none_p_kernel(
@@ -34,25 +37,25 @@ def tile_picked_pinball_none_p_kernel(
         offs_sb = keep.tile([P, S // GROUP], U16, name="offs_sb")
         obs_sb = keep.tile([P, S // GROUP], U16, name="obs_sb")
         at_sb = keep.tile([P, S // GROUP], U16, name="at_sb")
-        scale_table = keep.tile([P, T], U8, name="scale_table", align_bytes=64)
+        scale_table = keep.tile([P, T], U8, name="scale_table", tag="scales_then_late", align_bytes=64)
         word_table = keep.tile([P, T], U32, name="word_table", align_bytes=64)
         x_planes = keep.tile([P, 2 * S], U8, name="x_planes", align_bytes=64)
+        raw_w2 = [keep.tile([P, PACK, N // 2], F32, name="raw_w2_%d" % h) for h in range(2)]
+        raw_w1_first = keep.tile([P, PACK, N // 2], F32, name="raw_w1_first")
+        w2_rows = w2.rearrange("(p j) (h c) -> p h j c", j=PACK, h=2)
+        w1_rows = w1.rearrange("(p j) (h c) -> p h j c", j=PACK, h=2)
+        tau_rows = tau.rearrange("(p t) s -> p t s", t=PACK)
 
         nc.gpsimd.memset(x_planes[:].bitcast(I32), 0)
-        nc.sync.dma_start(offs_sb[:], offs)
-        nc.sync.dma_start(obs_sb[:], obs)
         rows = x_scales[0].bitcast(I32)
         nc.sync.dma_start(scale_table[:].bitcast(I32), rows.unsqueeze(1).to_broadcast([16, 8, T // 4]))
-
-        raw = {}
-        raw["w2"] = keep.tile([P, PACK, N], F32, name="raw_w2", tag="w2_then_tau")
-        raw["w1"] = keep.tile([P, PACK, N], F32, name="raw_w1")
-        nc.sync.dma_start(raw["w2"][:], w2.rearrange("(p j) c -> p j c", j=PACK))
-        nc.sync.dma_start(word_table[:].bitcast(I32), x_words[0].rearrange("p c r -> p (c r)").bitcast(I32))
-        nc.sync.dma_start(raw["w1"][:], w1.rearrange("(p j) c -> p j c", j=PACK))
+        nc.sync.dma_start(obs_sb[:], obs)
+        nc.sync.dma_start(offs_sb[:], offs)
         nc.sync.dma_start(at_sb[:], at)
-        tau_rows = tau.rearrange("(p t) s -> p t s", t=PACK)
-        out_rows = out.rearrange("(p t) s -> p t s", t=PACK)
+        nc.sync.dma_start(word_table[:].bitcast(I32), x_words[0].rearrange("p c r -> p (c r)").bitcast(I32))
+        for h in range(2):
+            nc.sync.dma_start(raw_w2[h][:], w2_rows[:, h])
+        nc.sync.dma_start(raw_w1_first[:], w1_rows[:, 0])
 
         picked_scales = keep.tile([P, 2 * S], U8, name="picked_scales", align_bytes=64)
         e_words = keep.tile([P, S], U32, name="e_words", align_bytes=64)
@@ -60,25 +63,27 @@ def tile_picked_pinball_none_p_kernel(
         nc.vector.tensor_copy(picked_scales[:, :S], scale_table[:].indirect(obs_sb[:]))
         nc.vector.tensor_copy(picked_scales[:, S:], scale_table[:].indirect(offs_sb[:]))
         for r in range(PACK):
-            nc.scalar.dma_start(x_planes[:].bitcast(I32)[r:P:QUAD, :], picked_scales[:].bitcast(I32)[8 * r : P : QUAD, :])
+            nc.sync.dma_start(x_planes[:].bitcast(I32)[r:P:QUAD, :], picked_scales[:].bitcast(I32)[8 * r : P : QUAD, :])
+        late = keep.tile([P, PACK * (N // 2 + S)], F32, name="late", tag="scales_then_late", align_bytes=64)
+        raw_w1 = [raw_w1_first[:], late[:, : PACK * N // 2].rearrange("p (j c) -> p j c", j=PACK)]
+        tau_sb = late[:, PACK * N // 2 :].rearrange("p (t s) -> p t s", t=PACK)
+        nc.sync.dma_start(raw_w1[1], w1_rows[:, 1])
+        for u in range(2):
+            nc.sync.dma_start(tau_sb[:, 2 * u : 2 * u + 2, :], tau_rows[:, 2 * u : 2 * u + 2, :])
         nc.vector.tensor_copy(e_words[:], word_table[:].indirect(obs_sb[:]))
         nc.vector.tensor_copy(y_words[:], word_table[:].indirect(offs_sb[:]))
 
-        whole = slice(0, S)
-        halves = [slice(0, HALF), slice(HALF, S)]
+        def interleave(raw, grouped, first, on_vector):
+            src = raw.rearrange("p j (m t) -> p m j t", t=PACK)
+            dst = grouped[:].rearrange("p t m j -> p m j t")[:, first : first + src.shape[1]]
+            if on_vector > 0:
+                nc.vector.tensor_copy(dst[:, :on_vector], src[:, :on_vector])
+            if on_vector < src.shape[1]:
+                nc.scalar.copy(dst[:, on_vector:], src[:, on_vector:])
 
-        def y_pieces(t):
-            return [("y0", halves[0]), ("e0", halves[1])] if t == 0 else [("y%d" % t, whole)]
-
-        def product(name, words, scales, sign, pieces):
-            grouped = keep.tile([P, PACK, P, PACK], BF16, name="grouped_" + name, align_bytes=64)
+        def quantize(name, grouped):
             codes = keep.tile([P, N], U32, name="codes_" + name, align_bytes=64)
             planes = keep.tile([P, N], U8, name="planes_" + name, align_bytes=64)
-            dst = grouped[:].rearrange("p t m j -> p m j t")
-            src = raw[name][:].rearrange("p j (m t) -> p m j t", t=PACK)
-            nc.vector.tensor_copy(dst[:, :M_VECTOR], src[:, :M_VECTOR])
-            nc.scalar.copy(dst[:, M_VECTOR:], src[:, M_VECTOR:])
-            results = []
             for t in range(PACK):
                 cols = slice(P * t, P * (t + 1))
                 nc.vector.quantize_mx(
@@ -86,42 +91,58 @@ def tile_picked_pinball_none_p_kernel(
                     scales=planes[:, cols],
                     in_=grouped[:, t].rearrange("p m j -> p (m j)"),
                 )
-            for t in range(PACK):
-                cols = slice(P * t, P * (t + 1))
-                result = keep.tile([P, S], F32, name="res_%s_%d" % (name, t))
-                for bank, places in pieces(t):
-                    acc = psum.tile([P, places.stop - places.start], F32, name="acc", tag=bank)
-                    nc.tensor.matmul_mx(
-                        out=acc[:],
-                        lhsT=codes[:, cols].bitcast(FP8X4),
-                        lhsT_scale=planes[:, cols],
-                        rhs=words[:, places].bitcast(FP8X4),
-                        rhs_scale=scales[:, places],
-                        start=True,
-                        stop=True,
-                    )
-                    nc.scalar.activation(result[:, places], acc[:], COPY, scale=sign)
-                results.append(result)
-            return results
+            return codes, planes
 
-        neg_e = product("w2", e_words, x_planes[:, :S], -1.0, lambda t: [("e%d" % t, whole)])
-        tau_all = keep.tile([P, PACK, S], F32, name="tau_all", tag="w2_then_tau")
-        for u in range(2):
-            nc.sync.dma_start(tau_all[:, 2 * u : 2 * u + 2, :], tau_rows[:, 2 * u : 2 * u + 2, :])
-        tau_sb = [tau_all[:, t, :] for t in range(PACK)]
-        y = product("w1", y_words, x_planes[:, S:], 1.0, y_pieces)
+        grouped_w2 = keep.tile([P, PACK, P, PACK], BF16, name="grouped_w2", tag="grouped", align_bytes=64)
+        for h in range(2):
+            interleave(raw_w2[h][:], grouped_w2, M_HALF * h, W2_VECTOR[h])
+        w2_mx = quantize("w2", grouped_w2)
+        grouped_w1 = keep.tile([P, PACK, P, PACK], BF16, name="grouped_w1", tag="grouped", align_bytes=64)
+        for h in range(2):
+            interleave(raw_w1[h], grouped_w1, M_HALF * h, W1_VECTOR[h])
+        w1_mx = quantize("w1", grouped_w1)
 
+        whole = slice(0, S)
+        halves = [slice(0, HALF), slice(HALF, S)]
+
+        def product(result, weights, t, words, scales, places, bank, sign):
+            codes, planes = weights
+            cols = slice(P * t, P * (t + 1))
+            acc = psum.tile([P, places.stop - places.start], F32, name="acc", tag=bank)
+            nc.tensor.matmul_mx(
+                out=acc[:],
+                lhsT=codes[:, cols].bitcast(FP8X4),
+                lhsT_scale=planes[:, cols],
+                rhs=words[:, places].bitcast(FP8X4),
+                rhs_scale=scales[:, places],
+                start=True,
+                stop=True,
+            )
+            nc.scalar.activation(result[:, places], acc[:], COPY, scale=sign)
+
+        neg_e = [keep.tile([P, S], F32, name="neg_e_%d" % t) for t in range(PACK)]
+        y = [keep.tile([P, S], F32, name="y_%d" % t) for t in range(PACK)]
+        for t in range(PACK):
+            product(neg_e[t], w2_mx, t, e_words, x_planes[:, :S], whole, E_BANKS[t], -1.0)
+            if t == 0:
+                product(y[t], w1_mx, t, y_words, x_planes[:, S:], halves[0], E_BANKS[2], 1.0)
+                product(y[t], w1_mx, t, y_words, x_planes[:, S:], halves[1], E_BANKS[3], 1.0)
+            else:
+                product(y[t], w1_mx, t, y_words, x_planes[:, S:], whole, "y%d" % t, 1.0)
+
+        out_rows = out.rearrange("(p t) s -> p t s", t=PACK)
         miss = [keep.tile([P, S], F32, name="miss_%d" % t) for t in range(PACK)]
         tilt = [keep.tile([P, S], F32, name="tilt_%d" % t) for t in range(PACK)]
         loss = [keep.tile([P, S], F32, name="loss_%d" % t) for t in range(PACK)]
 
         def gather(t, h):
-            cols = slice(HALF * h, HALF * (h + 1))
             entries = at_sb[:, HALF // GROUP * h : HALF // GROUP * (h + 1)]
-            nc.vector.tensor_tensor(miss[t][:, cols], neg_e[t][:].indirect(entries), y[t][:, cols], ALU.add)
+            nc.vector.tensor_tensor(
+                miss[t][:, halves[h]], neg_e[t][:].indirect(entries), y[t][:, halves[h]], ALU.add
+            )
 
         def weigh(t, cols):
-            nc.vector.tensor_tensor(tilt[t][:, cols], miss[t][:, cols], tau_sb[t][:, cols], ALU.mult)
+            nc.vector.tensor_tensor(tilt[t][:, cols], miss[t][:, cols], tau_sb[:, t, cols], ALU.mult)
 
         def finish(t, cols):
             nc.vector.scalar_tensor_tensor(

@@ -21,9 +21,12 @@ QUAD = 32
 GROUP = 16
 HALF = S // 2
 M_HALF = P // 2
-W2_VECTOR = (0, 44)
-W1_VECTOR = (64, 64)
-E_BANKS = ("e0", "e1", "e2", "e3")
+W2_VECTOR = (0, 10)
+W1_VECTOR = (16, 16)
+W1_CUTS = (0, 256, 512)
+V_ALL = 32
+E_BANKS = ("b0", "b1", "b2", "b3")
+Y_BANKS = ("b2", "b3", "b4", "b5", "b6")
 
 
 def tile_picked_pinball_none_p_kernel(
@@ -41,10 +44,10 @@ def tile_picked_pinball_none_p_kernel(
         word_table = keep.tile([P, T], U32, name="word_table", align_bytes=64)
         x_planes = keep.tile([P, 2 * S], U8, name="x_planes", align_bytes=64)
         raw_w2 = [keep.tile([P, PACK, N // 2], F32, name="raw_w2_%d" % h) for h in range(2)]
-        raw_w1_first = keep.tile([P, PACK, N // 2], F32, name="raw_w1_first")
+        raw_w1_first = keep.tile([P, PACK, W1_CUTS[1]], F32, name="raw_w1_first")
         w2_rows = w2.rearrange("(p j) (h c) -> p h j c", j=PACK, h=2)
-        w1_rows = w1.rearrange("(p j) (h c) -> p h j c", j=PACK, h=2)
-        tau_rows = tau.rearrange("(p t) s -> p t s", t=PACK)
+        w1_rows = w1.rearrange("(p j) c -> p j c", j=PACK)
+        tau_rows = tau.rearrange("(v t i) s -> t v i s", t=PACK, i=PACK)
 
         nc.gpsimd.memset(x_planes[:].bitcast(I32), 0)
         rows = x_scales[0].bitcast(I32)
@@ -55,7 +58,7 @@ def tile_picked_pinball_none_p_kernel(
         nc.sync.dma_start(word_table[:].bitcast(I32), x_words[0].rearrange("p c r -> p (c r)").bitcast(I32))
         for h in range(2):
             nc.sync.dma_start(raw_w2[h][:], w2_rows[:, h])
-        nc.sync.dma_start(raw_w1_first[:], w1_rows[:, 0])
+        nc.sync.dma_start(raw_w1_first[:], w1_rows[:, :, : W1_CUTS[1]])
 
         picked_scales = keep.tile([P, 2 * S], U8, name="picked_scales", align_bytes=64)
         e_words = keep.tile([P, S], U32, name="e_words", align_bytes=64)
@@ -64,43 +67,46 @@ def tile_picked_pinball_none_p_kernel(
         nc.vector.tensor_copy(picked_scales[:, S:], scale_table[:].indirect(offs_sb[:]))
         for r in range(PACK):
             nc.sync.dma_start(x_planes[:].bitcast(I32)[r:P:QUAD, :], picked_scales[:].bitcast(I32)[8 * r : P : QUAD, :])
-        late = keep.tile([P, PACK * (N // 2 + S)], F32, name="late", tag="scales_then_late", align_bytes=64)
-        raw_w1 = [raw_w1_first[:], late[:, : PACK * N // 2].rearrange("p (j c) -> p j c", j=PACK)]
-        tau_sb = late[:, PACK * N // 2 :].rearrange("p (t s) -> p t s", t=PACK)
-        nc.sync.dma_start(raw_w1[1], w1_rows[:, 1])
-        for u in range(2):
-            nc.sync.dma_start(tau_sb[:, 2 * u : 2 * u + 2, :], tau_rows[:, 2 * u : 2 * u + 2, :])
+        late = keep.tile([P, PACK * (N - W1_CUTS[1] + S)], F32, name="late", tag="scales_then_late", align_bytes=64)
+        raw_w1 = [raw_w1_first[:]]
+        for lo, hi in zip(W1_CUTS[1:], W1_CUTS[2:]):
+            piece = late[:, PACK * (lo - W1_CUTS[1]) : PACK * (hi - W1_CUTS[1])].rearrange("p (j c) -> p j c", j=PACK)
+            nc.sync.dma_start(piece, w1_rows[:, :, lo:hi])
+            raw_w1.append(piece)
+        tau_sb = late[:, PACK * (N - W1_CUTS[1]) :].rearrange("p (t s) -> p t s", t=PACK)
+        for t in range(PACK):
+            nc.sync.dma_start(tau_sb[:, t, :], tau_rows[t])
         nc.vector.tensor_copy(e_words[:], word_table[:].indirect(obs_sb[:]))
         nc.vector.tensor_copy(y_words[:], word_table[:].indirect(offs_sb[:]))
 
         def interleave(raw, grouped, first, on_vector):
-            src = raw.rearrange("p j (m t) -> p m j t", t=PACK)
-            dst = grouped[:].rearrange("p t m j -> p m j t")[:, first : first + src.shape[1]]
+            src = raw.rearrange("p j (v t i) -> p v t j i", t=PACK, i=PACK)
+            dst = grouped[:].rearrange("p t (v i) j -> p v t j i", i=PACK)[:, first : first + src.shape[1]]
             if on_vector > 0:
                 nc.vector.tensor_copy(dst[:, :on_vector], src[:, :on_vector])
             if on_vector < src.shape[1]:
                 nc.scalar.copy(dst[:, on_vector:], src[:, on_vector:])
 
-        def quantize(name, grouped):
+        def quantize(name, grouped, runs):
             codes = keep.tile([P, N], U32, name="codes_" + name, align_bytes=64)
             planes = keep.tile([P, N], U8, name="planes_" + name, align_bytes=64)
-            for t in range(PACK):
-                cols = slice(P * t, P * (t + 1))
+            for lo, hi in runs:
+                cols = slice(P * lo, P * hi)
                 nc.vector.quantize_mx(
                     out=codes[:, cols].bitcast(FP8X4),
                     scales=planes[:, cols],
-                    in_=grouped[:, t].rearrange("p m j -> p (m j)"),
+                    in_=grouped[:, lo:hi].rearrange("p t m j -> p (t m j)"),
                 )
             return codes, planes
 
         grouped_w2 = keep.tile([P, PACK, P, PACK], BF16, name="grouped_w2", tag="grouped", align_bytes=64)
         for h in range(2):
-            interleave(raw_w2[h][:], grouped_w2, M_HALF * h, W2_VECTOR[h])
-        w2_mx = quantize("w2", grouped_w2)
+            interleave(raw_w2[h][:], grouped_w2, V_ALL // 2 * h, W2_VECTOR[h])
+        w2_mx = quantize("w2", grouped_w2, ((0, 1), (1, 2), (2, 4)))
         grouped_w1 = keep.tile([P, PACK, P, PACK], BF16, name="grouped_w1", tag="grouped", align_bytes=64)
-        for h in range(2):
-            interleave(raw_w1[h], grouped_w1, M_HALF * h, W1_VECTOR[h])
-        w1_mx = quantize("w1", grouped_w1)
+        for h in range(len(raw_w1)):
+            interleave(raw_w1[h], grouped_w1, W1_CUTS[h] // GROUP, W1_VECTOR[h])
+        w1_mx = quantize("w1", grouped_w1, ((0, 1), (1, 2), (2, 4)))
 
         whole = slice(0, S)
         halves = [slice(0, HALF), slice(HALF, S)]
@@ -120,44 +126,48 @@ def tile_picked_pinball_none_p_kernel(
             )
             nc.scalar.activation(result[:, places], acc[:], COPY, scale=sign)
 
-        neg_e = [keep.tile([P, S], F32, name="neg_e_%d" % t) for t in range(PACK)]
-        y = [keep.tile([P, S], F32, name="y_%d" % t) for t in range(PACK)]
+        windows = [keep.tile([P, S if t == 0 else 2 * S], F32, name="window_%d" % t) for t in range(PACK)]
+        y_last = keep.tile([P, S], F32, name="y_last")
+        neg_e = [windows[t][:, :S] for t in range(PACK)]
+        y = [windows[t + 1][:, S:] for t in range(PACK - 1)] + [y_last[:]]
         for t in range(PACK):
             product(neg_e[t], w2_mx, t, e_words, x_planes[:, :S], whole, E_BANKS[t], -1.0)
             if t == 0:
-                product(y[t], w1_mx, t, y_words, x_planes[:, S:], halves[0], E_BANKS[2], 1.0)
-                product(y[t], w1_mx, t, y_words, x_planes[:, S:], halves[1], E_BANKS[3], 1.0)
+                product(y[t], w1_mx, t, y_words, x_planes[:, S:], halves[0], Y_BANKS[0], 1.0)
+                product(y[t], w1_mx, t, y_words, x_planes[:, S:], halves[1], Y_BANKS[1], 1.0)
             else:
-                product(y[t], w1_mx, t, y_words, x_planes[:, S:], whole, "y%d" % t, 1.0)
+                product(y[t], w1_mx, t, y_words, x_planes[:, S:], whole, Y_BANKS[t + 1], 1.0)
 
-        out_rows = out.rearrange("(p t) s -> p t s", t=PACK)
-        miss = [keep.tile([P, S], F32, name="miss_%d" % t) for t in range(PACK)]
-        tilt = [keep.tile([P, S], F32, name="tilt_%d" % t) for t in range(PACK)]
-        loss = [keep.tile([P, S], F32, name="loss_%d" % t) for t in range(PACK)]
+        out_rows = out.rearrange("(v t i) s -> t v i s", t=PACK, i=PACK)
+        miss = keep.tile([P, PACK, S], F32, name="miss")
+        tilt = keep.tile([P, PACK, S], F32, name="tilt")
+        loss = keep.tile([P, PACK, S], F32, name="loss")
 
-        def gather(t, h):
-            entries = at_sb[:, HALF // GROUP * h : HALF // GROUP * (h + 1)]
-            nc.vector.tensor_tensor(
-                miss[t][:, halves[h]], neg_e[t][:].indirect(entries), y[t][:, halves[h]], ALU.add
-            )
+        def gather(t, cols):
+            entries = at_sb[:, cols.start // GROUP : cols.stop // GROUP]
+            nc.vector.tensor_tensor(miss[:, t, cols], windows[t][:].indirect(entries), y[t][:, cols], ALU.add)
 
-        def weigh(t, cols):
-            nc.vector.tensor_tensor(tilt[t][:, cols], miss[t][:, cols], tau_sb[:, t, cols], ALU.mult)
+        def weigh(tiles, cols):
+            nc.vector.tensor_tensor(tilt[:, tiles, cols], miss[:, tiles, cols], tau_sb[:, tiles, cols], ALU.mult)
 
-        def finish(t, cols):
+        def finish(tiles, cols):
             nc.vector.scalar_tensor_tensor(
-                loss[t][:, cols], miss[t][:, cols], 0.0, tilt[t][:, cols], ALU.max, ALU.subtract
+                loss[:, tiles, cols], miss[:, tiles, cols], 0.0, tilt[:, tiles, cols], ALU.max, ALU.subtract
             )
-            nc.sync.dma_start(out_rows[:, t, cols], loss[t][:, cols])
+            for t in range(tiles.start, tiles.stop):
+                nc.sync.dma_start(out_rows[t][:, :, cols], loss[:, t, cols])
 
-        gather(0, 0)
-        gather(0, 1)
-        for t in range(1, PACK):
-            gather(t, 0)
-            weigh(t - 1, whole)
-            gather(t, 1)
-            finish(t - 1, whole)
         for cols in halves:
-            weigh(PACK - 1, cols)
+            gather(0, cols)
+        gather(1, whole)
+        weigh(slice(0, 1), whole)
+        gather(2, whole)
+        weigh(slice(1, 2), whole)
+        finish(slice(0, 1), whole)
+        gather(3, whole)
+        finish(slice(1, 2), whole)
+        weigh(slice(2, 3), whole)
+        weigh(slice(3, 4), whole)
+        finish(slice(2, 3), whole)
         for cols in halves:
-            finish(PACK - 1, cols)
+            finish(slice(3, 4), cols)

@@ -1,6 +1,7 @@
 from contextlib import ExitStack
 
 import concourse.mybir as mybir
+from concourse.masks import make_identity
 
 K, T, S, N = 512, 2048, 512, 512
 FLOPS = 2 * 2 * K * N * S
@@ -14,19 +15,14 @@ U8 = mybir.dt.uint8
 FP8X4 = mybir.dt.float8_e4m3fn_x4
 ALU = mybir.AluOpType
 COPY = mybir.ActivationFunctionType.Copy
+RELU = mybir.ActivationFunctionType.Relu
 
 P = 128
 PACK = 4
 QUAD = 32
 GROUP = 16
 HALF = S // 2
-M_HALF = P // 2
-W2_VECTOR = (0, 10)
-W1_VECTOR = (16, 16)
-W1_CUTS = (0, 256, 512)
 V_ALL = 32
-E_BANKS = ("b0", "b1", "b2", "b3")
-Y_BANKS = ("b2", "b3", "b4", "b5", "b6")
 
 
 def tile_picked_pinball_none_p_kernel(
@@ -42,132 +38,183 @@ def tile_picked_pinball_none_p_kernel(
         at_sb = keep.tile([P, S // GROUP], U16, name="at_sb")
         scale_table = keep.tile([P, T], U8, name="scale_table", tag="scales_then_late", align_bytes=64)
         word_table = keep.tile([P, T], U32, name="word_table", align_bytes=64)
-        x_planes = keep.tile([P, 2 * S], U8, name="x_planes", align_bytes=64)
-        raw_w2 = [keep.tile([P, PACK, N // 2], F32, name="raw_w2_%d" % h) for h in range(2)]
-        raw_w1_first = keep.tile([P, PACK, W1_CUTS[1]], F32, name="raw_w1_first")
-        w2_rows = w2.rearrange("(p j) (h c) -> p h j c", j=PACK, h=2)
-        w1_rows = w1.rearrange("(p j) c -> p j c", j=PACK)
+        e_plane = keep.tile([P, S], U8, name="e_plane", align_bytes=64)
+        y_plane = keep.tile([P, S], U8, name="y_plane", align_bytes=64)
+        raw_w1 = keep.tile([P, PACK * N], F32, name="raw_w1")
         tau_rows = tau.rearrange("(v t i) s -> t v i s", t=PACK, i=PACK)
+        out_rows = out.rearrange("(v t i) s -> t v i s", t=PACK, i=PACK)
+        windows = [keep.tile([P, 2 * S if t < PACK - 1 else S], F32, name="window_%d" % t) for t in range(PACK)]
 
-        nc.gpsimd.memset(x_planes[:].bitcast(I32), 0)
+        nc.gpsimd.memset(e_plane[:].bitcast(I32), 0)
+        nc.gpsimd.memset(y_plane[:].bitcast(I32), 0)
+        nc.gpsimd.memset(windows[0][:, S:], 0.0)
+        identity = keep.tile([P, P], F32, name="identity")
+        make_identity(nc, identity[:])
         rows = x_scales[0].bitcast(I32)
         nc.sync.dma_start(scale_table[:].bitcast(I32), rows.unsqueeze(1).to_broadcast([16, 8, T // 4]))
-        nc.sync.dma_start(obs_sb[:], obs)
         nc.sync.dma_start(offs_sb[:], offs)
-        nc.sync.dma_start(at_sb[:], at)
+        nc.sync.dma_start(obs_sb[:], obs)
         nc.sync.dma_start(word_table[:].bitcast(I32), x_words[0].rearrange("p c r -> p (c r)").bitcast(I32))
-        for h in range(2):
-            nc.sync.dma_start(raw_w2[h][:], w2_rows[:, h])
-        nc.sync.dma_start(raw_w1_first[:], w1_rows[:, :, : W1_CUTS[1]])
+        nc.sync.dma_start(raw_w1[:], w1.rearrange("(p j) c -> p (j c)", j=PACK))
 
-        picked_scales = keep.tile([P, 2 * S], U8, name="picked_scales", align_bytes=64)
+        e_picked = keep.tile([P, S], U8, name="e_picked", align_bytes=64)
+        y_picked = keep.tile([P, S], U8, name="y_picked", tag="picked_then_tau", align_bytes=64)
         e_words = keep.tile([P, S], U32, name="e_words", align_bytes=64)
         y_words = keep.tile([P, S], U32, name="y_words", align_bytes=64)
-        nc.vector.tensor_copy(picked_scales[:, :S], scale_table[:].indirect(obs_sb[:]))
-        nc.vector.tensor_copy(picked_scales[:, S:], scale_table[:].indirect(offs_sb[:]))
-        for r in range(PACK):
-            nc.sync.dma_start(x_planes[:].bitcast(I32)[r:P:QUAD, :], picked_scales[:].bitcast(I32)[8 * r : P : QUAD, :])
-        late = keep.tile([P, PACK * (N - W1_CUTS[1] + S)], F32, name="late", tag="scales_then_late", align_bytes=64)
-        raw_w1 = [raw_w1_first[:]]
-        for lo, hi in zip(W1_CUTS[1:], W1_CUTS[2:]):
-            piece = late[:, PACK * (lo - W1_CUTS[1]) : PACK * (hi - W1_CUTS[1])].rearrange("p (j c) -> p j c", j=PACK)
-            nc.sync.dma_start(piece, w1_rows[:, :, lo:hi])
-            raw_w1.append(piece)
-        tau_sb = late[:, PACK * (N - W1_CUTS[1]) :].rearrange("p (t s) -> p t s", t=PACK)
-        for t in range(PACK):
-            nc.sync.dma_start(tau_sb[:, t, :], tau_rows[t])
-        nc.vector.tensor_copy(e_words[:], word_table[:].indirect(obs_sb[:]))
-        nc.vector.tensor_copy(y_words[:], word_table[:].indirect(offs_sb[:]))
+        e_scales, y_scales = e_plane[:], y_plane[:]
 
-        def interleave(raw, grouped, first, on_vector):
-            src = raw.rearrange("p j (v t i) -> p v t j i", t=PACK, i=PACK)
-            dst = grouped[:].rearrange("p t (v i) j -> p v t j i", i=PACK)[:, first : first + src.shape[1]]
+        def place(plane, picked):
+            for r in range(PACK):
+                nc.sync.dma_start(plane.bitcast(I32)[r:P:QUAD, :], picked[:].bitcast(I32)[8 * r : P : QUAD, :])
+
+        nc.vector.tensor_copy(y_picked[:], scale_table[:].indirect(offs_sb[:]))
+        place(y_scales, y_picked)
+        nc.vector.tensor_copy(e_picked[:], scale_table[:].indirect(obs_sb[:]))
+        raw_w2 = keep.tile([P, PACK * N], F32, name="raw_w2", tag="scales_then_late", align_bytes=64)[:]
+        nc.sync.dma_start(raw_w2, w2.rearrange("(p j) c -> p (j c)", j=PACK))
+        place(e_scales, e_picked)
+        nc.sync.dma_start(at_sb[:], at)
+        late = keep.tile([P, PACK * S], F32, name="late", tag="picked_then_tau", align_bytes=64)
+        tau_sb = [late[:, S * t : S * (t + 1)] for t in range(PACK)]
+        for t in range(PACK):
+            nc.sync.dma_start(tau_sb[t], tau_rows[t])
+        nc.vector.tensor_copy(y_words[:], word_table[:].indirect(offs_sb[:]))
+        nc.vector.tensor_copy(e_words[:], word_table[:].indirect(obs_sb[:]))
+
+        def stage(tag, count=1):
+            return keep.tile([P, count * P * PACK], BF16, name="grouped", tag=tag, align_bytes=64)[:]
+
+        def interleave(grouped, raw, t, on_vector):
+            src = raw.rearrange("p (j v t i) -> p t v j i", j=PACK, t=PACK, i=PACK)[:, t]
+            dst = grouped.rearrange("p (v i j) -> p v j i", i=PACK, j=PACK)
             if on_vector > 0:
                 nc.vector.tensor_copy(dst[:, :on_vector], src[:, :on_vector])
-            if on_vector < src.shape[1]:
+            if on_vector < V_ALL:
                 nc.scalar.copy(dst[:, on_vector:], src[:, on_vector:])
+            return grouped
 
-        def quantize(name, grouped, runs):
-            codes = keep.tile([P, N], U32, name="codes_" + name, align_bytes=64)
-            planes = keep.tile([P, N], U8, name="planes_" + name, align_bytes=64)
-            for lo, hi in runs:
-                cols = slice(P * lo, P * hi)
-                nc.vector.quantize_mx(
-                    out=codes[:, cols].bitcast(FP8X4),
-                    scales=planes[:, cols],
-                    in_=grouped[:, lo:hi].rearrange("p t m j -> p (t m j)"),
-                )
-            return codes, planes
-
-        grouped_w2 = keep.tile([P, PACK, P, PACK], BF16, name="grouped_w2", tag="grouped", align_bytes=64)
-        for h in range(2):
-            interleave(raw_w2[h][:], grouped_w2, V_ALL // 2 * h, W2_VECTOR[h])
-        w2_mx = quantize("w2", grouped_w2, ((0, 1), (1, 2), (2, 4)))
-        grouped_w1 = keep.tile([P, PACK, P, PACK], BF16, name="grouped_w1", tag="grouped", align_bytes=64)
-        for h in range(len(raw_w1)):
-            interleave(raw_w1[h], grouped_w1, W1_CUTS[h] // GROUP, W1_VECTOR[h])
-        w1_mx = quantize("w1", grouped_w1, ((0, 1), (1, 2), (2, 4)))
+        def quantize(name, grouped):
+            width = grouped.shape[1] // PACK
+            codes = keep.tile([P, width], U32, name="codes_" + name, align_bytes=64)
+            planes = keep.tile([P, width], U8, name="planes_" + name, align_bytes=64)
+            nc.vector.quantize_mx(out=codes[:].bitcast(FP8X4), scales=planes[:], in_=grouped)
+            return [(codes[:, c : c + P], planes[:, c : c + P]) for c in range(0, width, P)]
 
         whole = slice(0, S)
         halves = [slice(0, HALF), slice(HALF, S)]
+        blocks = [slice(c, c + P) for c in range(0, S, P)]
 
-        def product(result, weights, t, words, scales, places, bank, sign):
+        def bank(number, width=S):
+            return psum.tile([P, width], F32, name="acc", tag="bank_%d" % number)
+
+        def product(weights, words, scales, places, number):
             codes, planes = weights
-            cols = slice(P * t, P * (t + 1))
-            acc = psum.tile([P, places.stop - places.start], F32, name="acc", tag=bank)
+            acc = bank(number, places.stop - places.start)
             nc.tensor.matmul_mx(
                 out=acc[:],
-                lhsT=codes[:, cols].bitcast(FP8X4),
-                lhsT_scale=planes[:, cols],
+                lhsT=codes.bitcast(FP8X4),
+                lhsT_scale=planes,
                 rhs=words[:, places].bitcast(FP8X4),
                 rhs_scale=scales[:, places],
                 start=True,
                 stop=True,
             )
-            nc.scalar.activation(result[:, places], acc[:], COPY, scale=sign)
+            return acc
 
-        windows = [keep.tile([P, S if t == 0 else 2 * S], F32, name="window_%d" % t) for t in range(PACK)]
-        y_last = keep.tile([P, S], F32, name="y_last")
+        def turn(acc, src, start=True, stop=True):
+            for b, cols in enumerate(blocks):
+                nc.tensor.matmul(
+                    acc[:, cols], src[:, cols], identity[:],
+                    start=start and b == 0, stop=stop and b == len(blocks) - 1, is_transpose=True,
+                )
+            return acc
+
         neg_e = [windows[t][:, :S] for t in range(PACK)]
-        y = [windows[t + 1][:, S:] for t in range(PACK - 1)] + [y_last[:]]
+        y_own = [keep.tile([P, S], F32, name="y_%d" % t) for t in (2, 3)]
+        y = [windows[1][:, S:], windows[2][:, S:], y_own[0][:], y_own[1][:]]
+        miss = [keep.tile([P, S], F32, name="miss", tag="miss_%d" % t) for t in range(2)]
+
+        def entries(cols):
+            return at_sb[:, cols.start // GROUP : cols.stop // GROUP]
+
+        def e_out(t, weights, places, number):
+            acc = product(weights, e_words, e_scales, places, number)
+            nc.scalar.activation(neg_e[t][:, places], acc[:], COPY, scale=-1.0)
+
+        def y_out(t, weights, number):
+            acc = product(weights, y_words, y_scales, whole, number)
+            nc.scalar.copy(y[t], acc[:])
+
+        def gather(t, cols=whole):
+            nc.vector.tensor_tensor(miss[t][:, cols], windows[t][:].indirect(entries(cols)), y[t][:, cols], ALU.add)
+
+        def weigh(t, tilt, cols):
+            nc.vector.tensor_tensor(tilt[:, cols], miss[t][:, cols], tau_sb[t][:, cols], ALU.mult)
+
+        def finish(t, loss, tilt, cols):
+            nc.vector.scalar_tensor_tensor(loss[:, cols], miss[t][:, cols], 0.0, tilt[:, cols], ALU.max, ALU.subtract)
+
+        def plain(name, tag=None):
+            return keep.tile([P, S], F32, name="plain", tag=tag or name)
+
+        width = P * PACK
+        g1 = [interleave(stage("stage_w1_%d" % t), raw_w1[:], t, V_ALL if t in (1, 2) else 0) for t in range(PACK)]
         for t in range(PACK):
-            product(neg_e[t], w2_mx, t, e_words, x_planes[:, :S], whole, E_BANKS[t], -1.0)
-            if t == 0:
-                product(y[t], w1_mx, t, y_words, x_planes[:, S:], halves[0], Y_BANKS[0], 1.0)
-                product(y[t], w1_mx, t, y_words, x_planes[:, S:], halves[1], Y_BANKS[1], 1.0)
-            else:
-                product(y[t], w1_mx, t, y_words, x_planes[:, S:], whole, Y_BANKS[t + 1], 1.0)
+            y_out(t, quantize("w1_%d" % t, g1[t])[0], 2 + t)
 
-        out_rows = out.rearrange("(v t i) s -> t v i s", t=PACK, i=PACK)
-        miss = keep.tile([P, PACK, S], F32, name="miss")
-        tilt = keep.tile([P, PACK, S], F32, name="tilt")
-        loss = keep.tile([P, PACK, S], F32, name="loss")
+        q2 = quantize("w2_0", interleave(stage("stage_w2"), raw_w2, 0, V_ALL))
+        for h, cols in enumerate(halves):
+            acc = product(q2[0], e_words, e_scales, cols, h)
+            nc.vector.tensor_scalar(neg_e[0][:, cols], acc[:], -1.0, None, ALU.mult)
+        rest = stage("stage_w2", PACK - 1)
+        for t in range(1, PACK):
+            interleave(rest[:, width * (t - 1) : width * t], raw_w2, t, V_ALL)
+        q2 = q2 + quantize("w2_12", rest[:, : 2 * width]) + quantize("w2_3", rest[:, 2 * width :])
+        turned_tau = []
+        for t in range(2):
+            acc = turn(bank(t), tau_sb[t])
+            pieces = [keep.tile([P, HALF], F32, name="piece", tag=tag) for tag in ("miss_%d" % (t + 2), "tau_%d" % t)]
+            for piece, cols in zip(pieces, halves):
+                nc.scalar.activation(piece[:], acc[:, cols], COPY, scale=-1.0)
+            turned_tau.append(pieces)
+        for t in range(1, PACK):
+            e_out(t, q2[t], whole, 1 + t)
 
-        def gather(t, cols):
-            entries = at_sb[:, cols.start // GROUP : cols.stop // GROUP]
-            nc.vector.tensor_tensor(miss[:, t, cols], windows[t][:].indirect(entries), y[t][:, cols], ALU.add)
+        def turn_back(t, tilt, above, number):
+            acc = turn(turn(bank(number), tilt, stop=False), above, start=False)
+            loss = plain("loss_%d" % t)
+            nc.scalar.copy(loss[:], acc[:])
+            nc.sync.dma_start(out_rows[t], loss[:])
 
-        def weigh(tiles, cols):
-            nc.vector.tensor_tensor(tilt[:, tiles, cols], miss[:, tiles, cols], tau_sb[:, tiles, cols], ALU.mult)
+        gather(0)
+        turned = turn(bank(5), miss[0])
+        gather(1)
+        tilt, above = plain("tilt_0"), plain("above_0")
+        for piece, cols in zip(turned_tau[0], halves):
+            nc.vector.tensor_tensor(tilt[:, cols], turned[:, cols], piece[:], ALU.mult)
+        nc.scalar.activation(above[:], turned[:], RELU)
+        for_vector = turn(bank(6), miss[1])
+        for_scalar = turn(bank(7), miss[1])
+        miss.append(plain("miss_2"))
+        gather(2)
+        turn_back(0, tilt, above, 0)
+        tilt, above = plain("tilt_1"), plain("above_1")
+        nc.scalar.activation(above[:], for_scalar[:], RELU)
+        for piece, cols in zip(turned_tau[1], halves):
+            nc.vector.tensor_tensor(tilt[:, cols], for_vector[:, cols], piece[:], ALU.mult)
+        miss.append(plain("miss_3"))
+        turn_back(1, tilt, above, 1)
 
-        def finish(tiles, cols):
-            nc.vector.scalar_tensor_tensor(
-                loss[:, tiles, cols], miss[:, tiles, cols], 0.0, tilt[:, tiles, cols], ALU.max, ALU.subtract
-            )
-            for t in range(tiles.start, tiles.stop):
-                nc.sync.dma_start(out_rows[t][:, :, cols], loss[:, t, cols])
-
+        tilt = plain("tilt_2", "miss_1")
+        weigh(2, tilt, whole)
+        gather(3, halves[0])
+        loss = plain("loss_2")
+        finish(2, loss, tilt, whole)
+        nc.sync.dma_start(out_rows[2], loss[:])
+        gather(3, halves[1])
+        tilt, loss = plain("tilt_3"), plain("loss_3")
         for cols in halves:
-            gather(0, cols)
-        gather(1, whole)
-        weigh(slice(0, 1), whole)
-        gather(2, whole)
-        weigh(slice(1, 2), whole)
-        finish(slice(0, 1), whole)
-        gather(3, whole)
-        finish(slice(1, 2), whole)
-        weigh(slice(2, 3), whole)
-        weigh(slice(3, 4), whole)
-        finish(slice(2, 3), whole)
+            weigh(3, tilt, cols)
         for cols in halves:
-            finish(slice(3, 4), cols)
+            finish(3, loss, tilt, cols)
+            nc.sync.dma_start(out_rows[3][:, :, cols], loss[:, cols])

@@ -159,14 +159,15 @@ def tile_picked_pinball_none_p_kernel(
 
         width = P * PACK
         g1 = [interleave(stage("stage_w1_%d" % t), raw_w1[:], t, V_ALL if t in (1, 2) else 0) for t in range(PACK)]
-        for t in range(PACK):
-            y_out(t, quantize("w1_%d" % t, g1[t])[0], 2 + t)
+        q1 = [quantize("w1_%d" % t, g1[t])[0] for t in range(PACK)]
+        for t in range(PACK - 1):
+            y_out(t, q1[t], 2 + t)
 
         q2 = quantize("w2_0", interleave(stage("stage_w2"), raw_w2, 0, V_ALL))
-        for h, cols in enumerate(halves):
-            acc = product(q2[0], e_words, e_scales, cols, h)
-            nc.vector.tensor_scalar(neg_e[0][:, cols], acc[:], -1.0, None, ALU.mult)
-        rest = stage("stage_w2", PACK - 1)
+        e_out(0, q2[0], halves[0], 0)
+        acc = product(q2[0], e_words, e_scales, halves[1], 1)
+        nc.vector.tensor_scalar(neg_e[0][:, halves[1]], acc[:], -1.0, None, ALU.mult)
+        rest = stage("stage_w2_rest", PACK - 1)
         for t in range(1, PACK):
             interleave(rest[:, width * (t - 1) : width * t], raw_w2, t, V_ALL)
         q2 = q2 + quantize("w2_12", rest[:, : 2 * width]) + quantize("w2_3", rest[:, 2 * width :])
@@ -179,6 +180,7 @@ def tile_picked_pinball_none_p_kernel(
             turned_tau.append(pieces)
         for t in range(1, PACK):
             e_out(t, q2[t], whole, 1 + t)
+        y_out(PACK - 1, q1[PACK - 1], 2)
 
         def turn_back(t, tilt, above, number):
             acc = turn(turn(bank(number), tilt, stop=False), above, start=False)

@@ -58,7 +58,7 @@ def tile_picked_pinball_none_p_kernel(
         nc.sync.dma_start(raw_w1[:], w1.rearrange("(p j) c -> p (j c)", j=PACK))
 
         e_picked = keep.tile([P, S], U8, name="e_picked", align_bytes=64)
-        y_picked = keep.tile([P, S], U8, name="y_picked", tag="picked_then_tau", align_bytes=64)
+        y_picked = keep.tile([P, S], U8, name="y_picked", align_bytes=64)
         e_words = keep.tile([P, S], U32, name="e_words", align_bytes=64)
         y_words = keep.tile([P, S], U32, name="y_words", align_bytes=64)
         e_scales, y_scales = e_plane[:], y_plane[:]
@@ -70,13 +70,14 @@ def tile_picked_pinball_none_p_kernel(
         nc.vector.tensor_copy(y_picked[:], scale_table[:].indirect(offs_sb[:]))
         place(y_scales, y_picked)
         nc.vector.tensor_copy(e_picked[:], scale_table[:].indirect(obs_sb[:]))
-        raw_w2 = keep.tile([P, PACK * N], F32, name="raw_w2", tag="scales_then_late", align_bytes=64)[:]
+        late = keep.tile([P, PACK * (N + S)], F32, name="late", tag="scales_then_late", align_bytes=64)
+        raw_w2 = late[:, : PACK * N]
         nc.sync.dma_start(raw_w2, w2.rearrange("(p j) c -> p (j c)", j=PACK))
+        tau_sb = [late[:, PACK * N + S * t : PACK * N + S * (t + 1)] for t in range(PACK)]
+        nc.sync.dma_start(tau_sb[0], tau_rows[0])
         place(e_scales, e_picked)
         nc.sync.dma_start(at_sb[:], at)
-        late = keep.tile([P, PACK * S], F32, name="late", tag="picked_then_tau", align_bytes=64)
-        tau_sb = [late[:, S * t : S * (t + 1)] for t in range(PACK)]
-        for t in range(PACK):
+        for t in range(1, PACK):
             nc.sync.dma_start(tau_sb[t], tau_rows[t])
         nc.vector.tensor_copy(y_words[:], word_table[:].indirect(offs_sb[:]))
         nc.vector.tensor_copy(e_words[:], word_table[:].indirect(obs_sb[:]))
@@ -93,9 +94,9 @@ def tile_picked_pinball_none_p_kernel(
                 nc.scalar.copy(dst[:, on_vector:], src[:, on_vector:])
             return grouped
 
-        def quantize(name, grouped):
+        def quantize(name, grouped, tag=None):
             width = grouped.shape[1] // PACK
-            codes = keep.tile([P, width], U32, name="codes_" + name, align_bytes=64)
+            codes = keep.tile([P, width], U32, name="codes", tag=tag or "codes_" + name, align_bytes=64)
             planes = keep.tile([P, width], U8, name="planes_" + name, align_bytes=64)
             nc.vector.quantize_mx(out=codes[:].bitcast(FP8X4), scales=planes[:], in_=grouped)
             return [(codes[:, c : c + P], planes[:, c : c + P]) for c in range(0, width, P)]
@@ -170,16 +171,16 @@ def tile_picked_pinball_none_p_kernel(
         rest = stage("stage_w2_rest", PACK - 1)
         for t in range(1, PACK):
             interleave(rest[:, width * (t - 1) : width * t], raw_w2, t, V_ALL)
-        q2 = q2 + quantize("w2_12", rest[:, : 2 * width]) + quantize("w2_3", rest[:, 2 * width :])
+        q2 = q2 + quantize("w2_12", rest[:, : 2 * width]) + quantize("w2_3", rest[:, 2 * width :], "codes_w2_0")
         turned_tau = []
         for t in range(2):
+            e_out(t + 1, q2[t + 1], whole, 2 + t)
             acc = turn(bank(t), tau_sb[t])
             pieces = [keep.tile([P, HALF], F32, name="piece", tag=tag) for tag in ("miss_%d" % (t + 2), "tau_%d" % t)]
             for piece, cols in zip(pieces, halves):
                 nc.scalar.activation(piece[:], acc[:, cols], COPY, scale=-1.0)
             turned_tau.append(pieces)
-        for t in range(1, PACK):
-            e_out(t, q2[t], whole, 1 + t)
+        e_out(PACK - 1, q2[PACK - 1], whole, 4)
         y_out(PACK - 1, q1[PACK - 1], 2)
 
         def turn_back(t, tilt, above, number):

@@ -161,7 +161,7 @@ def tile_picked_pinball_none_p_kernel(
         width = P * PACK
         g1 = [interleave(stage("stage_w1_%d" % t), raw_w1[:], t, V_ALL if t in (1, 2) else 0) for t in range(PACK)]
         q1 = [quantize("w1_%d" % t, g1[t])[0] for t in range(PACK)]
-        for t in range(PACK - 1):
+        for t in range(2):
             y_out(t, q1[t], 2 + t)
 
         q2 = quantize("w2_0", interleave(stage("stage_w2"), raw_w2, 0, V_ALL))
@@ -175,19 +175,19 @@ def tile_picked_pinball_none_p_kernel(
         turned_tau = []
         for t in range(2):
             e_out(t + 1, q2[t + 1], whole, 2 + t)
-            acc = turn(bank(t), tau_sb[t])
+            acc = turn(bank(4 * t), tau_sb[t])
             pieces = [keep.tile([P, HALF], F32, name="piece", tag=tag) for tag in ("miss_%d" % (t + 2), "tau_%d" % t)]
             for piece, cols in zip(pieces, halves):
                 nc.scalar.activation(piece[:], acc[:, cols], COPY, scale=-1.0)
             turned_tau.append(pieces)
-        e_out(PACK - 1, q2[PACK - 1], whole, 4)
-        y_out(PACK - 1, q1[PACK - 1], 2)
+            if t == 0:
+                y_out(2, q1[2], 1)
 
         def turn_back(t, tilt, above, number):
             acc = turn(turn(bank(number), tilt, stop=False), above, start=False)
             loss = plain("loss_%d" % t)
             nc.scalar.copy(loss[:], acc[:])
-            nc.sync.dma_start(out_rows[t], loss[:])
+            nc.scalar.dma_start(out_rows[t], loss[:])
 
         gather(0)
         turned = turn(bank(5), miss[0])
@@ -196,6 +196,8 @@ def tile_picked_pinball_none_p_kernel(
         for piece, cols in zip(turned_tau[0], halves):
             nc.vector.tensor_tensor(tilt[:, cols], turned[:, cols], piece[:], ALU.mult)
         nc.scalar.activation(above[:], turned[:], RELU)
+        e_out(PACK - 1, q2[PACK - 1], whole, 2)
+        y_out(PACK - 1, q1[PACK - 1], 1)
         for_vector = turn(bank(6), miss[1])
         for_scalar = turn(bank(7), miss[1])
         miss.append(plain("miss_2"))

@@ -159,8 +159,8 @@ def tile_picked_pinball_none_p_kernel(
             return keep.tile([P, S], F32, name="plain", tag=tag or name)
 
         width = P * PACK
-        g1 = [interleave(stage("stage_w1_%d" % t), raw_w1[:], t, V_ALL if t in (1, 2) else 0) for t in range(PACK)]
-        q1 = [quantize("w1_%d" % t, g1[t])[0] for t in range(PACK)]
+        g1 = [interleave(stage("stage_w1_%d" % t), raw_w1[:], t, 0) for t in range(PACK)]
+        q1 = [quantize("w1_%d" % t, g1[t])[0] for t in range(PACK - 1)]
         for t in range(2):
             y_out(t, q1[t], 2 + t)
 
@@ -168,6 +168,7 @@ def tile_picked_pinball_none_p_kernel(
         e_out(0, q2[0], halves[0], 0)
         acc = product(q2[0], e_words, e_scales, halves[1], 1)
         nc.vector.tensor_scalar(neg_e[0][:, halves[1]], acc[:], -1.0, None, ALU.mult)
+        q1 = q1 + quantize("w1_3", g1[PACK - 1], "stage_w2")
         rest = stage("stage_w2_rest", PACK - 1)
         for t in range(1, PACK):
             interleave(rest[:, width * (t - 1) : width * t], raw_w2, t, V_ALL)

@@ -159,7 +159,9 @@ def tile_picked_pinball_none_p_kernel(
             return keep.tile([P, S], F32, name="plain", tag=tag or name)
 
         width = P * PACK
-        g1 = [interleave(stage("stage_w1_%d" % t), raw_w1[:], t, 0) for t in range(PACK)]
+        g1 = [interleave(stage("stage_w1_%d" % t), raw_w1[:], t, 0) for t in range(PACK - 1)]
+        last = stage("stage_last", 2)
+        interleave(last[:, :width], raw_w1[:], PACK - 1, 0)
         q1 = [quantize("w1_%d" % t, g1[t])[0] for t in range(PACK - 1)]
         for t in range(2):
             y_out(t, q1[t], 2 + t)
@@ -168,11 +170,13 @@ def tile_picked_pinball_none_p_kernel(
         e_out(0, q2[0], halves[0], 0)
         acc = product(q2[0], e_words, e_scales, halves[1], 1)
         nc.vector.tensor_scalar(neg_e[0][:, halves[1]], acc[:], -1.0, None, ALU.mult)
-        q1 = q1 + quantize("w1_3", g1[PACK - 1], "stage_w2")
-        rest = stage("stage_w2_rest", PACK - 1)
-        for t in range(1, PACK):
-            interleave(rest[:, width * (t - 1) : width * t], raw_w2, t, V_ALL)
-        q2 = q2 + quantize("w2_12", rest[:, : 2 * width]) + quantize("w2_3", rest[:, 2 * width :], "codes_w2_0")
+        middle = stage("stage_w2_middle", 2)
+        for t in (1, 2):
+            interleave(middle[:, width * (t - 1) : width * t], raw_w2, t, V_ALL)
+        interleave(last[:, width:], raw_w2, PACK - 1, V_ALL)
+        q2 = q2 + quantize("w2_12", middle)
+        last_y, last_e = quantize("last", last, "codes_w2_0")
+        q1, q2 = q1 + [last_y], q2 + [last_e]
         turned_tau = []
         for t in range(2):
             e_out(t + 1, q2[t + 1], whole, 2 + t)

@@ -1,7 +1,6 @@
 from contextlib import ExitStack
 
 import concourse.mybir as mybir
-from concourse.masks import make_identity
 
 K, T, S, N = 512, 2048, 512, 512
 FLOPS = 2 * 2 * K * N * S
@@ -15,14 +14,12 @@ U8 = mybir.dt.uint8
 FP8X4 = mybir.dt.float8_e4m3fn_x4
 ALU = mybir.AluOpType
 COPY = mybir.ActivationFunctionType.Copy
-RELU = mybir.ActivationFunctionType.Relu
 
 P = 128
 PACK = 4
 QUAD = 32
 GROUP = 16
 HALF = S // 2
-V_ALL = 32
 
 
 def tile_picked_pinball_none_p_kernel(
@@ -36,195 +33,118 @@ def tile_picked_pinball_none_p_kernel(
         offs_sb = keep.tile([P, S // GROUP], U16, name="offs_sb")
         obs_sb = keep.tile([P, S // GROUP], U16, name="obs_sb")
         at_sb = keep.tile([P, S // GROUP], U16, name="at_sb")
-        scale_table = keep.tile([P, T], U8, name="scale_table", tag="scales_then_late", align_bytes=64)
-        word_table = keep.tile([P, T], U32, name="word_table", align_bytes=64)
+        scale_table = keep.tile([P, T], U8, name="scale_table", tag="scales_then_w1", align_bytes=64)
+        word_table = keep.tile([P, T], U32, name="word_table", tag="words_then_tau", align_bytes=64)
         e_plane = keep.tile([P, S], U8, name="e_plane", align_bytes=64)
         y_plane = keep.tile([P, S], U8, name="y_plane", align_bytes=64)
-        raw_w1 = keep.tile([P, PACK * N], F32, name="raw_w1")
+        raw_w2 = keep.tile([P, PACK * N], F32, name="raw_w2")
         tau_rows = tau.rearrange("(v t i) s -> t v i s", t=PACK, i=PACK)
         out_rows = out.rearrange("(v t i) s -> t v i s", t=PACK, i=PACK)
-        windows = [keep.tile([P, 2 * S if t < PACK - 1 else S], F32, name="window_%d" % t) for t in range(PACK)]
+        whole = slice(0, S)
+        halves = [slice(0, HALF), slice(HALF, S)]
 
-        nc.gpsimd.memset(e_plane[:].bitcast(I32), 0)
-        nc.gpsimd.memset(y_plane[:].bitcast(I32), 0)
-        nc.gpsimd.memset(windows[0][:, S:], 0.0)
-        identity = keep.tile([P, P], F32, name="identity")
-        make_identity(nc, identity[:])
+        def entries(list_sb, cols):
+            return list_sb[:, cols.start // GROUP : cols.stop // GROUP]
+
+        nc.vector.memset(e_plane[:].bitcast(I32), 0)
+        nc.vector.memset(y_plane[:].bitcast(I32), 0)
         rows = x_scales[0].bitcast(I32)
         nc.sync.dma_start(scale_table[:].bitcast(I32), rows.unsqueeze(1).to_broadcast([16, 8, T // 4]))
-        nc.sync.dma_start(offs_sb[:], offs)
         nc.sync.dma_start(obs_sb[:], obs)
+        nc.sync.dma_start(offs_sb[:], offs)
         nc.sync.dma_start(word_table[:].bitcast(I32), x_words[0].rearrange("p c r -> p (c r)").bitcast(I32))
-        nc.sync.dma_start(raw_w1[:], w1.rearrange("(p j) c -> p (j c)", j=PACK))
+        nc.sync.dma_start(raw_w2[:], w2.rearrange("(p j) c -> p (j c)", j=PACK))
+        nc.sync.dma_start(at_sb[:], at)
 
         e_picked = keep.tile([P, S], U8, name="e_picked", align_bytes=64)
         y_picked = keep.tile([P, S], U8, name="y_picked", align_bytes=64)
         e_words = keep.tile([P, S], U32, name="e_words", align_bytes=64)
-        y_words = keep.tile([P, S], U32, name="y_words", align_bytes=64)
-        e_scales, y_scales = e_plane[:], y_plane[:]
 
         def place(plane, picked):
             for r in range(PACK):
-                nc.sync.dma_start(plane.bitcast(I32)[r:P:QUAD, :], picked[:].bitcast(I32)[8 * r : P : QUAD, :])
+                nc.sync.dma_start(plane[:].bitcast(I32)[r:P:QUAD, :], picked[:].bitcast(I32)[8 * r : P : QUAD, :])
 
-        nc.vector.tensor_copy(y_picked[:], scale_table[:].indirect(offs_sb[:]))
-        place(y_scales, y_picked)
+        def pick_y_words(half, tag):
+            words = keep.tile([P, HALF], U32, name="y_words", tag=tag, align_bytes=64)
+            nc.vector.tensor_copy(words[:], word_table[:].indirect(entries(offs_sb, halves[half])))
+            return words
+
         nc.vector.tensor_copy(e_picked[:], scale_table[:].indirect(obs_sb[:]))
-        late = keep.tile([P, PACK * (N + S)], F32, name="late", tag="scales_then_late", align_bytes=64)
-        raw_w2 = late[:, : PACK * N]
-        nc.sync.dma_start(raw_w2, w2.rearrange("(p j) c -> p (j c)", j=PACK))
-        tau_sb = [late[:, PACK * N + S * t : PACK * N + S * (t + 1)] for t in range(PACK)]
-        nc.sync.dma_start(tau_sb[0], tau_rows[0])
-        place(e_scales, e_picked)
-        nc.sync.dma_start(at_sb[:], at)
-        for t in range(1, PACK):
-            nc.sync.dma_start(tau_sb[t], tau_rows[t])
-        nc.vector.tensor_copy(y_words[:], word_table[:].indirect(offs_sb[:]))
+        place(e_plane, e_picked)
+        nc.vector.tensor_copy(y_picked[:], scale_table[:].indirect(offs_sb[:]))
+        raw_w1 = keep.tile([P, PACK * N], F32, name="raw_w1", tag="scales_then_w1", align_bytes=64)
+        nc.sync.dma_start(raw_w1[:], w1.rearrange("(p j) c -> p (j c)", j=PACK))
+        place(y_plane, y_picked)
         nc.vector.tensor_copy(e_words[:], word_table[:].indirect(obs_sb[:]))
+        y_words = [pick_y_words(0, "y_words")]
 
-        def stage(tag, count=1):
-            return keep.tile([P, count * P * PACK], BF16, name="grouped", tag=tag, align_bytes=64)[:]
-
-        def interleave(grouped, raw, t, on_vector):
-            src = raw.rearrange("p (j v t i) -> p t v j i", j=PACK, t=PACK, i=PACK)[:, t]
-            dst = grouped.rearrange("p (v i j) -> p v j i", i=PACK, j=PACK)
-            if on_vector > 0:
-                nc.vector.tensor_copy(dst[:, :on_vector], src[:, :on_vector])
-            if on_vector < V_ALL:
-                nc.scalar.copy(dst[:, on_vector:], src[:, on_vector:])
+        def interleave(tag, raw, t, engine_copy):
+            grouped = keep.tile([P, P * PACK], BF16, name="grouped", tag=tag, align_bytes=64)
+            src = raw[:].rearrange("p (j v t i) -> p t v j i", j=PACK, t=PACK, i=PACK)[:, t]
+            engine_copy(grouped[:].rearrange("p (v i j) -> p v j i", i=PACK, j=PACK), src)
             return grouped
 
-        def quantize(name, grouped, tag=None):
-            width = grouped.shape[1] // PACK
-            codes = keep.tile([P, width], U32, name="codes", tag=tag or "codes_" + name, align_bytes=64)
-            planes = keep.tile([P, width], U8, name="planes_" + name, align_bytes=64)
-            nc.vector.quantize_mx(out=codes[:].bitcast(FP8X4), scales=planes[:], in_=grouped)
-            return [(codes[:, c : c + P], planes[:, c : c + P]) for c in range(0, width, P)]
-
-        whole = slice(0, S)
-        halves = [slice(0, HALF), slice(HALF, S)]
-        blocks = [slice(c, c + P) for c in range(0, S, P)]
+        def quantize(name, grouped):
+            codes = keep.tile([P, P], U32, name="codes_" + name, align_bytes=64)
+            planes = keep.tile([P, P], U8, name="planes_" + name, align_bytes=64)
+            nc.vector.quantize_mx(out=codes[:].bitcast(FP8X4), scales=planes[:], in_=grouped[:])
+            return codes, planes
 
         def bank(number, width=S):
             return psum.tile([P, width], F32, name="acc", tag="bank_%d" % number)
 
-        def product(weights, words, scales, places, number):
+        def product(acc, weights, words, scales):
             codes, planes = weights
-            acc = bank(number, places.stop - places.start)
             nc.tensor.matmul_mx(
-                out=acc[:],
-                lhsT=codes.bitcast(FP8X4),
-                lhsT_scale=planes,
-                rhs=words[:, places].bitcast(FP8X4),
-                rhs_scale=scales[:, places],
+                out=acc,
+                lhsT=codes[:].bitcast(FP8X4),
+                lhsT_scale=planes[:],
+                rhs=words.bitcast(FP8X4),
+                rhs_scale=scales,
                 start=True,
                 stop=True,
             )
             return acc
 
-        def turn(acc, src, start=True, stop=True):
-            for b, cols in enumerate(blocks):
-                nc.tensor.matmul(
-                    acc[:, cols], src[:, cols], identity[:],
-                    start=start and b == 0, stop=stop and b == len(blocks) - 1, is_transpose=True,
-                )
-            return acc
+        def plain(name):
+            return keep.tile([P, S], F32, name=name)
 
-        neg_e = [windows[t][:, :S] for t in range(PACK)]
-        y_own = [keep.tile([P, S], F32, name="y_%d" % t) for t in (2, 3)]
-        y = [windows[1][:, S:], windows[2][:, S:], y_own[0][:], y_own[1][:]]
-        miss = [keep.tile([P, S], F32, name="miss", tag="miss_%d" % t) for t in range(2)]
+        on_vector, on_scalar = nc.vector.tensor_copy, nc.scalar.copy
+        g2 = [interleave("stage_%d" % t, raw_w2, t, on_vector if t < 2 else on_scalar) for t in range(PACK)]
+        q2 = [quantize("w2_%d" % t, g2[t]) for t in range(2)]
+        y_words.append(pick_y_words(1, "stage_0"))
+        tau_all = keep.tile([P, PACK * S], F32, name="tau_all", tag="words_then_tau", align_bytes=64)
+        tau_sb = [tau_all[:, S * t : S * (t + 1)] for t in range(PACK)]
+        for t in range(PACK):
+            nc.sync.dma_start(tau_sb[t], tau_rows[t])
+        q2 = q2 + [quantize("w2_%d" % t, g2[t]) for t in range(2, PACK)]
+        target = []
+        for t in range(PACK):
+            window = keep.tile([P, S], F32, name="window", tag="window_%d" % (t % 2))
+            for number, cols in ((0, halves[0]), (7, halves[1])) if t == 0 else ((t, whole),):
+                acc = bank(number, cols.stop - cols.start)
+                on_scalar(window[:, cols], product(acc[:], q2[t], e_words[:, cols], e_plane[:, cols]))
+            picked = plain("target_%d" % t)
+            for cols in halves:
+                nc.scalar.activation(picked[:, cols], window[:].indirect(entries(at_sb, cols)), COPY)
+            target.append(picked)
 
-        def entries(cols):
-            return at_sb[:, cols.start // GROUP : cols.stop // GROUP]
-
-        def e_out(t, weights, places, number):
-            acc = product(weights, e_words, e_scales, places, number)
-            nc.scalar.activation(neg_e[t][:, places], acc[:], COPY, scale=-1.0)
-
-        def y_out(t, weights, number):
-            acc = product(weights, y_words, y_scales, whole, number)
-            nc.scalar.copy(y[t], acc[:])
-
-        def gather(t, cols=whole):
-            nc.vector.tensor_tensor(miss[t][:, cols], windows[t][:].indirect(entries(cols)), y[t][:, cols], ALU.add)
-
-        def weigh(t, tilt, cols):
-            nc.vector.tensor_tensor(tilt[:, cols], miss[t][:, cols], tau_sb[t][:, cols], ALU.mult)
-
-        def finish(t, loss, tilt, cols):
-            nc.vector.scalar_tensor_tensor(loss[:, cols], miss[t][:, cols], 0.0, tilt[:, cols], ALU.max, ALU.subtract)
-
-        def plain(name, tag=None):
-            return keep.tile([P, S], F32, name="plain", tag=tag or name)
-
-        width = P * PACK
-        g1 = [interleave(stage("stage_w1_%d" % t), raw_w1[:], t, 0) for t in range(PACK - 1)]
-        last = stage("stage_last", 2)
-        interleave(last[:, :width], raw_w1[:], PACK - 1, 0)
-        q1 = [quantize("w1_%d" % t, g1[t])[0] for t in range(PACK - 1)]
-        for t in range(2):
-            y_out(t, q1[t], 2 + t)
-
-        q2 = quantize("w2_0", interleave(stage("stage_w2"), raw_w2, 0, V_ALL))
-        e_out(0, q2[0], halves[0], 0)
-        acc = product(q2[0], e_words, e_scales, halves[1], 1)
-        nc.vector.tensor_scalar(neg_e[0][:, halves[1]], acc[:], -1.0, None, ALU.mult)
-        middle = stage("stage_w2_middle", 2)
-        for t in (1, 2):
-            interleave(middle[:, width * (t - 1) : width * t], raw_w2, t, V_ALL)
-        interleave(last[:, width:], raw_w2, PACK - 1, V_ALL)
-        q2 = q2 + quantize("w2_12", middle)
-        last_y, last_e = quantize("last", last, "codes_w2_0")
-        q1, q2 = q1 + [last_y], q2 + [last_e]
-        turned_tau = []
-        for t in range(2):
-            e_out(t + 1, q2[t + 1], whole, 2 + t)
-            acc = turn(bank(4 * t), tau_sb[t])
-            pieces = [keep.tile([P, HALF], F32, name="piece", tag=tag) for tag in ("miss_%d" % (t + 2), "tau_%d" % t)]
-            for piece, cols in zip(pieces, halves):
-                nc.scalar.activation(piece[:], acc[:, cols], COPY, scale=-1.0)
-            turned_tau.append(pieces)
-            if t == 0:
-                y_out(2, q1[2], 1)
-
-        def turn_back(t, tilt, above, number):
-            acc = turn(turn(bank(number), tilt, stop=False), above, start=False)
-            loss = plain("loss_%d" % t)
-            nc.scalar.copy(loss[:], acc[:])
-            nc.scalar.dma_start(out_rows[t], loss[:])
-
-        gather(0)
-        turned = turn(bank(5), miss[0])
-        gather(1)
-        tilt, above = plain("tilt_0"), plain("above_0")
-        for piece, cols in zip(turned_tau[0], halves):
-            nc.vector.tensor_tensor(tilt[:, cols], turned[:, cols], piece[:], ALU.mult)
-        nc.scalar.activation(above[:], turned[:], RELU)
-        e_out(PACK - 1, q2[PACK - 1], whole, 2)
-        y_out(PACK - 1, q1[PACK - 1], 1)
-        for_vector = turn(bank(6), miss[1])
-        for_scalar = turn(bank(7), miss[1])
-        miss.append(plain("miss_2"))
-        gather(2)
-        turn_back(0, tilt, above, 0)
-        tilt, above = plain("tilt_1"), plain("above_1")
-        nc.scalar.activation(above[:], for_scalar[:], RELU)
-        for piece, cols in zip(turned_tau[1], halves):
-            nc.vector.tensor_tensor(tilt[:, cols], for_vector[:, cols], piece[:], ALU.mult)
-        miss.append(plain("miss_3"))
-        turn_back(1, tilt, above, 1)
-
-        tilt = plain("tilt_2", "miss_1")
-        weigh(2, tilt, whole)
-        gather(3, halves[0])
-        loss = plain("loss_2")
-        finish(2, loss, tilt, whole)
-        nc.sync.dma_start(out_rows[2], loss[:])
-        gather(3, halves[1])
-        tilt, loss = plain("tilt_3"), plain("loss_3")
-        for cols in halves:
-            weigh(3, tilt, cols)
-        for cols in halves:
-            finish(3, loss, tilt, cols)
-            nc.sync.dma_start(out_rows[3][:, :, cols], loss[:, cols])
+        y = []
+        for t in range(PACK):
+            weights = quantize("w1_%d" % t, interleave("stage_%d" % (t + 1), raw_w1, t, on_vector))
+            acc = bank(PACK + t)
+            for half, cols in enumerate(halves):
+                product(acc[:, cols], weights, y_words[half][:], y_plane[:, cols])
+            y.append(acc)
+        for t in range(PACK):
+            miss, tilt, loss = plain("miss_%d" % t), plain("tilt_%d" % t), plain("loss_%d" % t)
+            pieces = halves if t in (0, PACK - 1) else [whole]
+            for cols in halves:
+                nc.vector.tensor_tensor(miss[:, cols], y[t][:, cols], target[t][:, cols], ALU.subtract)
+            for cols in pieces:
+                nc.vector.tensor_tensor(tilt[:, cols], miss[:, cols], tau_sb[t][:, cols], ALU.mult)
+            for cols in pieces:
+                nc.vector.scalar_tensor_tensor(loss[:, cols], miss[:, cols], 0.0, tilt[:, cols], ALU.max, ALU.subtract)
+                if cols.stop == S or t == PACK - 1:
+                    done = cols if t == PACK - 1 else whole
+                    nc.sync.dma_start(out_rows[t][:, :, done], loss[:, done])

@@ -30,10 +30,11 @@ def tile_picked_pinball_none_p_kernel(
         keep = ctx.enter_context(tc.tile_pool(name="keep", bufs=1))
         psum = ctx.enter_context(tc.psum_pool(name="psum", bufs=1))
 
+        late = ctx.enter_context(tc.tile_pool(name="late", bufs=1))
         offs_sb = keep.tile([P, S // GROUP], U16, name="offs_sb")
         obs_sb = keep.tile([P, S // GROUP], U16, name="obs_sb")
         at_sb = keep.tile([P, S // GROUP], U16, name="at_sb")
-        scale_table = keep.tile([P, T], U8, name="scale_table", tag="scales_then_w1", align_bytes=64)
+        scale_table = late.tile([P, T], U8, name="scale_table", offset=0, align_bytes=64)
         word_table = keep.tile([P, T], U32, name="word_table", tag="words_then_tau", align_bytes=64)
         e_plane = keep.tile([P, S], U8, name="e_plane", align_bytes=64)
         y_plane = keep.tile([P, S], U8, name="y_plane", align_bytes=64)
@@ -72,7 +73,7 @@ def tile_picked_pinball_none_p_kernel(
         nc.vector.tensor_copy(e_picked[:], scale_table[:].indirect(obs_sb[:]))
         place(e_plane, e_picked)
         nc.vector.tensor_copy(y_picked[:], scale_table[:].indirect(offs_sb[:]))
-        raw_w1 = keep.tile([P, PACK * N], F32, name="raw_w1", tag="scales_then_w1", align_bytes=64)
+        raw_w1 = late.tile([P, PACK * N], F32, name="raw_w1", offset=0, align_bytes=64)
         nc.sync.dma_start(raw_w1[:], w1.rearrange("(p j) c -> p (j c)", j=PACK))
         place(y_plane, y_picked)
         nc.vector.tensor_copy(e_words[:], word_table[:].indirect(obs_sb[:]))
@@ -84,8 +85,8 @@ def tile_picked_pinball_none_p_kernel(
             engine_copy(grouped[:].rearrange("p (v i j) -> p v j i", i=PACK, j=PACK), src)
             return grouped
 
-        def quantize(name, grouped):
-            codes = keep.tile([P, P], U32, name="codes_" + name, align_bytes=64)
+        def quantize(name, grouped, tag=None):
+            codes = keep.tile([P, P], U32, name="codes", tag=tag or "codes_" + name, align_bytes=64)
             planes = keep.tile([P, P], U8, name="planes_" + name, align_bytes=64)
             nc.vector.quantize_mx(out=codes[:].bitcast(FP8X4), scales=planes[:], in_=grouped[:])
             return codes, planes
@@ -107,7 +108,7 @@ def tile_picked_pinball_none_p_kernel(
             return acc
 
         def plain(name):
-            return keep.tile([P, S], F32, name=name)
+            return keep.tile([P, S], F32, name=name, align_bytes=64)
 
         on_vector, on_scalar = nc.vector.tensor_copy, nc.scalar.copy
         g2 = [interleave("stage_%d" % t, raw_w2, t, on_vector if t < 2 else on_scalar) for t in range(PACK)]
@@ -118,33 +119,56 @@ def tile_picked_pinball_none_p_kernel(
         for t in range(PACK):
             nc.sync.dma_start(tau_sb[t], tau_rows[t])
         q2 = q2 + [quantize("w2_%d" % t, g2[t]) for t in range(2, PACK)]
-        target = []
-        for t in range(PACK):
-            window = keep.tile([P, S], F32, name="window", tag="window_%d" % (t % 2))
-            for number, cols in ((0, halves[0]), (7, halves[1])) if t == 0 else ((t, whole),):
-                acc = bank(number, cols.stop - cols.start)
-                on_scalar(window[:, cols], product(acc[:], q2[t], e_words[:, cols], e_plane[:, cols]))
-            picked = plain("target_%d" % t)
-            for cols in halves:
-                nc.scalar.activation(picked[:, cols], window[:].indirect(entries(at_sb, cols)), COPY)
-            target.append(picked)
 
-        y = []
-        for t in range(PACK):
-            weights = quantize("w1_%d" % t, interleave("stage_%d" % (t + 1), raw_w1, t, on_vector))
+        def empty_e(t, window):
+            for number, cols in zip(((0, 7), (1, 6))[t], halves) if t < 2 else ((t, whole),):
+                acc = bank(number, cols.stop - cols.start)
+                (on_vector if t == 1 else on_scalar)(window[:, cols], product(acc[:], q2[t], e_words[:, cols], e_plane[:, cols]))
+            return window
+
+        def fetch(picked, window, cols):
+            nc.scalar.activation(picked[:, cols], window[:].indirect(entries(at_sb, cols)), COPY)
+
+        def forecast(t, grouped, tag=None):
+            weights = quantize("w1_%d" % t, grouped, tag)
             acc = bank(PACK + t)
             for half, cols in enumerate(halves):
                 product(acc[:, cols], weights, y_words[half][:], y_plane[:, cols])
-            y.append(acc)
-        for t in range(PACK):
-            miss, tilt, loss = plain("miss_%d" % t), plain("tilt_%d" % t), plain("loss_%d" % t)
-            pieces = halves if t in (0, PACK - 1) else [whole]
+            return acc
+
+        target = []
+        for t in range(2):
+            window = empty_e(t, keep.tile([P, S], F32, name="window", tag="window_%d" % t))
+            target.append(plain("target_%d" % t))
             for cols in halves:
-                nc.vector.tensor_tensor(miss[:, cols], y[t][:, cols], target[t][:, cols], ALU.subtract)
-            for cols in pieces:
-                nc.vector.tensor_tensor(tilt[:, cols], miss[:, cols], tau_sb[t][:, cols], ALU.mult)
-            for cols in pieces:
-                nc.vector.scalar_tensor_tensor(loss[:, cols], miss[:, cols], 0.0, tilt[:, cols], ALU.max, ALU.subtract)
-                if cols.stop == S or t == PACK - 1:
-                    done = cols if t == PACK - 1 else whole
-                    nc.sync.dma_start(out_rows[t][:, :, done], loss[:, done])
+                fetch(target[t], window, cols)
+        window = empty_e(2, keep.tile([P, S], F32, name="window", tag="window_0"))
+        y = [forecast(t, interleave("stage_%d" % (t + 1), raw_w1, t, on_vector)) for t in range(PACK - 1)]
+        last_grouped = interleave("stage_4", raw_w1, PACK - 1, on_scalar)
+        target.append(late.tile([P, S], F32, name="target_2", offset=0, align_bytes=64))
+        target.append(plain("target_3"))
+        fetch(target[2], window, halves[0])
+        last_window = empty_e(3, late.tile([P, S], F32, name="window_3", offset=4 * S, align_bytes=64))
+        fetch(target[2], window, halves[1])
+        for cols in halves:
+            fetch(target[3], last_window, cols)
+        miss = [plain("miss_%d" % t) for t in range(PACK)]
+        tilt = [plain("tilt_%d" % t) for t in range(PACK)]
+        loss = [plain("loss_%d" % t) for t in range(PACK)]
+        steps = [(t, cols) for t in range(PACK) for cols in halves]
+
+        def finish(t, cols):
+            nc.vector.scalar_tensor_tensor(loss[t][:, cols], miss[t][:, cols], 0.0, tilt[t][:, cols], ALU.max, ALU.subtract)
+            if t == PACK - 1:
+                nc.sync.dma_start(out_rows[t][:, :, cols], loss[t][:, cols])
+            elif cols.stop == S:
+                nc.sync.dma_start(out_rows[t], loss[t][:])
+
+        for n, (t, cols) in enumerate(steps):
+            nc.vector.tensor_tensor(miss[t][:, cols], y[t][:, cols], target[t][:, cols], ALU.subtract)
+            if n > 0:
+                finish(*steps[n - 1])
+            if n == 2:
+                y.append(forecast(PACK - 1, last_grouped, "miss_0"))
+            nc.vector.tensor_tensor(tilt[t][:, cols], miss[t][:, cols], tau_sb[t][:, cols], ALU.mult)
+        finish(*steps[-1])

@@ -20,6 +20,7 @@ PACK = 4
 QUAD = 32
 GROUP = 16
 HALF = S // 2
+V_ALL = P // PACK
 
 
 def tile_picked_pinball_none_p_kernel(
@@ -79,10 +80,14 @@ def tile_picked_pinball_none_p_kernel(
         nc.vector.tensor_copy(e_words[:], word_table[:].indirect(obs_sb[:]))
         y_words = [pick_y_words(0, "y_words")]
 
-        def interleave(tag, raw, t, engine_copy):
+        def interleave(tag, raw, t, on_vector):
             grouped = keep.tile([P, P * PACK], BF16, name="grouped", tag=tag, align_bytes=64)
             src = raw[:].rearrange("p (j v t i) -> p t v j i", j=PACK, t=PACK, i=PACK)[:, t]
-            engine_copy(grouped[:].rearrange("p (v i j) -> p v j i", i=PACK, j=PACK), src)
+            dst = grouped[:].rearrange("p (v i j) -> p v j i", i=PACK, j=PACK)
+            if on_vector > 0:
+                nc.vector.tensor_copy(dst[:, :on_vector], src[:, :on_vector])
+            if on_vector < V_ALL:
+                nc.scalar.copy(dst[:, on_vector:], src[:, on_vector:])
             return grouped
 
         def quantize(name, grouped, tag=None):
@@ -111,7 +116,7 @@ def tile_picked_pinball_none_p_kernel(
             return keep.tile([P, S], F32, name=name, align_bytes=64)
 
         on_vector, on_scalar = nc.vector.tensor_copy, nc.scalar.copy
-        g2 = [interleave("stage_%d" % t, raw_w2, t, on_vector if t < 2 else on_scalar) for t in range(PACK)]
+        g2 = [interleave("stage_%d" % t, raw_w2, t, V_ALL if t < 2 else 0) for t in range(PACK)]
         q2 = [quantize("w2_%d" % t, g2[t]) for t in range(2)]
         y_words.append(pick_y_words(1, "stage_0"))
         tau_all = keep.tile([P, PACK * S], F32, name="tau_all", tag="words_then_tau", align_bytes=64)
@@ -143,8 +148,8 @@ def tile_picked_pinball_none_p_kernel(
             for cols in halves:
                 fetch(target[t], window, cols)
         window = empty_e(2, keep.tile([P, S], F32, name="window", tag="window_0"))
-        y = [forecast(t, interleave("stage_%d" % (t + 1), raw_w1, t, on_vector)) for t in range(PACK - 1)]
-        last_grouped = interleave("stage_4", raw_w1, PACK - 1, on_scalar)
+        y = [forecast(t, interleave("stage_%d" % (t + 1), raw_w1, t, V_ALL)) for t in range(PACK - 1)]
+        last_grouped = interleave("stage_4", raw_w1, PACK - 1, V_ALL // 2)
         target.append(late.tile([P, S], F32, name="target_2", offset=0, align_bytes=64))
         target.append(plain("target_3"))
         fetch(target[2], window, halves[0])
@@ -155,7 +160,7 @@ def tile_picked_pinball_none_p_kernel(
         miss = [plain("miss_%d" % t) for t in range(PACK)]
         tilt = [plain("tilt_%d" % t) for t in range(PACK)]
         loss = [plain("loss_%d" % t) for t in range(PACK)]
-        steps = [(t, cols) for t in range(PACK) for cols in halves]
+        steps = [(t, cols) for t in range(PACK) for cols in ([whole] if t == 1 else halves)]
 
         def finish(t, cols):
             nc.vector.scalar_tensor_tensor(loss[t][:, cols], miss[t][:, cols], 0.0, tilt[t][:, cols], ALU.max, ALU.subtract)

@@ -128,7 +128,7 @@ def tile_picked_pinball_none_p_kernel(
         def empty_e(t, window):
             for number, cols in zip(((0, 7), (1, 6))[t], halves) if t < 2 else ((t, whole),):
                 acc = bank(number, cols.stop - cols.start)
-                (on_vector if t == 1 else on_scalar)(window[:, cols], product(acc[:], q2[t], e_words[:, cols], e_plane[:, cols]))
+                (on_vector if number == 1 else on_scalar)(window[:, cols], product(acc[:], q2[t], e_words[:, cols], e_plane[:, cols]))
             return window
 
         def fetch(picked, window, cols):
@@ -141,26 +141,18 @@ def tile_picked_pinball_none_p_kernel(
                 product(acc[:, cols], weights, y_words[half][:], y_plane[:, cols])
             return acc
 
-        target = []
-        for t in range(2):
-            window = empty_e(t, keep.tile([P, S], F32, name="window", tag="window_%d" % t))
-            target.append(plain("target_%d" % t))
-            for cols in halves:
-                fetch(target[t], window, cols)
-        window = empty_e(2, keep.tile([P, S], F32, name="window", tag="window_0"))
+        steps = [(t, cols) for t in range(PACK) for cols in halves]
+        target = [plain("target_%d" % t) for t in range(PACK)]
+        windows = [empty_e(t, keep.tile([P, S], F32, name="window", tag="window_%d" % t)) for t in range(2)]
+        for n, (t, cols) in enumerate(steps):
+            fetch(target[t], windows[t], cols)
+            if n in (2, 4):
+                windows.append(empty_e(t + 1, keep.tile([P, S], F32, name="window", tag="window_%d" % (t - 1))))
         y = [forecast(t, interleave("stage_%d" % (t + 1), raw_w1, t, V_ALL)) for t in range(PACK - 1)]
-        last_grouped = interleave("stage_4", raw_w1, PACK - 1, V_ALL // 2)
-        target.append(late.tile([P, S], F32, name="target_2", offset=0, align_bytes=64))
-        target.append(plain("target_3"))
-        fetch(target[2], window, halves[0])
-        last_window = empty_e(3, late.tile([P, S], F32, name="window_3", offset=4 * S, align_bytes=64))
-        fetch(target[2], window, halves[1])
-        for cols in halves:
-            fetch(target[3], last_window, cols)
+        last_grouped = interleave("stage_4", raw_w1, PACK - 1, V_ALL)
         miss = [plain("miss_%d" % t) for t in range(PACK)]
         tilt = [plain("tilt_%d" % t) for t in range(PACK)]
         loss = [plain("loss_%d" % t) for t in range(PACK)]
-        steps = [(t, cols) for t in range(PACK) for cols in ([whole] if t == 1 else halves)]
 
         def finish(t, cols):
             nc.vector.scalar_tensor_tensor(loss[t][:, cols], miss[t][:, cols], 0.0, tilt[t][:, cols], ALU.max, ALU.subtract)
@@ -171,9 +163,10 @@ def tile_picked_pinball_none_p_kernel(
 
         for n, (t, cols) in enumerate(steps):
             nc.vector.tensor_tensor(miss[t][:, cols], y[t][:, cols], target[t][:, cols], ALU.subtract)
-            if n > 0:
-                finish(*steps[n - 1])
-            if n == 2:
-                y.append(forecast(PACK - 1, last_grouped, "miss_0"))
+            if n > 1:
+                finish(*steps[n - 2])
+            if n == 3:
+                y.append(forecast(PACK - 1, last_grouped, "tilt_0"))
             nc.vector.tensor_tensor(tilt[t][:, cols], miss[t][:, cols], tau_sb[t][:, cols], ALU.mult)
-        finish(*steps[-1])
+        for step in steps[-2:]:
+            finish(*step)

@@ -20,7 +20,6 @@ PACK = 4
 QUAD = 32
 GROUP = 16
 HALF = S // 2
-V_ALL = P // PACK
 
 
 def tile_picked_pinball_none_p_kernel(
@@ -80,21 +79,18 @@ def tile_picked_pinball_none_p_kernel(
         nc.vector.tensor_copy(e_words[:], word_table[:].indirect(obs_sb[:]))
         y_words = [pick_y_words(0, "y_words")]
 
-        def interleave(tag, raw, t, on_vector):
-            grouped = keep.tile([P, P * PACK], BF16, name="grouped", tag=tag, align_bytes=64)
-            src = raw[:].rearrange("p (j v t i) -> p t v j i", j=PACK, t=PACK, i=PACK)[:, t]
-            dst = grouped[:].rearrange("p (v i j) -> p v j i", i=PACK, j=PACK)
-            if on_vector > 0:
-                nc.vector.tensor_copy(dst[:, :on_vector], src[:, :on_vector])
-            if on_vector < V_ALL:
-                nc.scalar.copy(dst[:, on_vector:], src[:, on_vector:])
+        def interleave(tag, raw, first, count, copy):
+            grouped = keep.tile([P, count * P * PACK], BF16, name="grouped", tag=tag, align_bytes=64)
+            src = raw[:].rearrange("p (j v t i) -> p t v j i", j=PACK, t=PACK, i=PACK)[:, first : first + count]
+            copy(grouped[:].rearrange("p (t v i j) -> p t v j i", t=count, i=PACK, j=PACK), src)
             return grouped
 
         def quantize(name, grouped, tag=None):
-            codes = keep.tile([P, P], U32, name="codes", tag=tag or "codes_" + name, align_bytes=64)
-            planes = keep.tile([P, P], U8, name="planes_" + name, align_bytes=64)
+            width = grouped.shape[1] // PACK
+            codes = keep.tile([P, width], U32, name="codes", tag=tag or "codes_" + name, align_bytes=64)
+            planes = keep.tile([P, width], U8, name="planes_" + name, align_bytes=64)
             nc.vector.quantize_mx(out=codes[:].bitcast(FP8X4), scales=planes[:], in_=grouped[:])
-            return codes, planes
+            return [(codes[:, c : c + P], planes[:, c : c + P]) for c in range(0, width, P)]
 
         def bank(number, width=S):
             return psum.tile([P, width], F32, name="acc", tag="bank_%d" % number)
@@ -103,8 +99,8 @@ def tile_picked_pinball_none_p_kernel(
             codes, planes = weights
             nc.tensor.matmul_mx(
                 out=acc,
-                lhsT=codes[:].bitcast(FP8X4),
-                lhsT_scale=planes[:],
+                lhsT=codes.bitcast(FP8X4),
+                lhsT_scale=planes,
                 rhs=words.bitcast(FP8X4),
                 rhs_scale=scales,
                 start=True,
@@ -116,31 +112,38 @@ def tile_picked_pinball_none_p_kernel(
             return keep.tile([P, S], F32, name=name, align_bytes=64)
 
         on_vector, on_scalar = nc.vector.tensor_copy, nc.scalar.copy
-        g2 = [interleave("stage_%d" % t, raw_w2, t, V_ALL if t < 2 else 0) for t in range(PACK)]
-        q2 = [quantize("w2_%d" % t, g2[t]) for t in range(2)]
+        q2 = [quantize("w2_%d" % t, interleave("stage_%d" % t, raw_w2, t, 1, on_vector))[0] for t in range(2)]
+        late_w2 = interleave("stage_2", raw_w2, 2, 2, on_scalar)
         y_words.append(pick_y_words(1, "stage_0"))
         tau_all = keep.tile([P, PACK * S], F32, name="tau_all", tag="words_then_tau", align_bytes=64)
         tau_sb = [tau_all[:, S * t : S * (t + 1)] for t in range(PACK)]
         for t in range(PACK):
             nc.sync.dma_start(tau_sb[t], tau_rows[t])
-        q2 = q2 + [quantize("w2_%d" % t, g2[t]) for t in range(2, PACK)]
+        q2 = q2 + quantize("w2_23", late_w2)
 
         def empty_e(t, window):
-            for number, cols in zip(((0, 7), (1, 6))[t], halves) if t < 2 else ((t, whole),):
+            for number, cols, copy in e_pieces[t]:
                 acc = bank(number, cols.stop - cols.start)
-                (on_vector if number == 1 else on_scalar)(window[:, cols], product(acc[:], q2[t], e_words[:, cols], e_plane[:, cols]))
+                copy(window[:, cols], product(acc[:], q2[t], e_words[:, cols], e_plane[:, cols]))
             return window
 
         def fetch(picked, window, cols):
             nc.scalar.activation(picked[:, cols], window[:].indirect(entries(at_sb, cols)), COPY)
 
-        def forecast(t, grouped, tag=None):
-            weights = quantize("w1_%d" % t, grouped, tag)
-            acc = bank(PACK + t)
-            for half, cols in enumerate(halves):
-                product(acc[:, cols], weights, y_words[half][:], y_plane[:, cols])
-            return acc
+        def forecast(t, weights):
+            if t == 0:
+                accs = [bank(number, HALF)[:] for number in (PACK, 0)]
+            else:
+                acc = bank(PACK + t)
+                accs = [acc[:, cols] for cols in halves]
+            return [product(accs[half], weights, y_words[half][:], y_plane[:, cols]) for half, cols in enumerate(halves)]
 
+        e_pieces = [
+            [(0, halves[0], on_scalar), (7, halves[1], on_scalar)],
+            [(1, halves[0], on_scalar), (5, slice(HALF, HALF + P), on_vector), (6, slice(HALF + P, S), on_vector)],
+            [(2, whole, on_scalar)],
+            [(3, whole, on_scalar)],
+        ]
         steps = [(t, cols) for t in range(PACK) for cols in halves]
         target = [plain("target_%d" % t) for t in range(PACK)]
         windows = [empty_e(t, keep.tile([P, S], F32, name="window", tag="window_%d" % t)) for t in range(2)]
@@ -148,8 +151,8 @@ def tile_picked_pinball_none_p_kernel(
             fetch(target[t], windows[t], cols)
             if n in (2, 4):
                 windows.append(empty_e(t + 1, keep.tile([P, S], F32, name="window", tag="window_%d" % (t - 1))))
-        y = [forecast(t, interleave("stage_%d" % (t + 1), raw_w1, t, V_ALL)) for t in range(PACK - 1)]
-        last_grouped = interleave("stage_4", raw_w1, PACK - 1, V_ALL)
+        y = [forecast(t, quantize("w1_%d" % t, interleave("stage_%d" % (t + 1), raw_w1, t, 1, on_vector))[0]) for t in range(3)]
+        late_w1 = interleave("stage_4", raw_w1, 3, 1, on_vector)
         miss = [plain("miss_%d" % t) for t in range(PACK)]
         tilt = [plain("tilt_%d" % t) for t in range(PACK)]
         loss = [plain("loss_%d" % t) for t in range(PACK)]
@@ -162,11 +165,11 @@ def tile_picked_pinball_none_p_kernel(
                 nc.sync.dma_start(out_rows[t], loss[t][:])
 
         for n, (t, cols) in enumerate(steps):
-            nc.vector.tensor_tensor(miss[t][:, cols], y[t][:, cols], target[t][:, cols], ALU.subtract)
+            nc.vector.tensor_tensor(miss[t][:, cols], y[t][n % 2], target[t][:, cols], ALU.subtract)
             if n > 1:
                 finish(*steps[n - 2])
             if n == 3:
-                y.append(forecast(PACK - 1, last_grouped, "tilt_0"))
+                y.append(forecast(PACK - 1, quantize("w1_3", late_w1, "tilt_0")[0]))
             nc.vector.tensor_tensor(tilt[t][:, cols], miss[t][:, cols], tau_sb[t][:, cols], ALU.mult)
         for step in steps[-2:]:
             finish(*step)

@@ -140,7 +140,7 @@ def tile_picked_pinball_none_p_kernel(
 
         e_pieces = [
             [(0, halves[0], on_scalar), (7, halves[1], on_scalar)],
-            [(1, halves[0], on_scalar), (5, slice(HALF, HALF + P), on_vector), (6, slice(HALF + P, S), on_vector)],
+            [(1, halves[0], on_scalar), (6, halves[1], on_scalar)],
             [(2, whole, on_scalar)],
             [(3, whole, on_scalar)],
         ]

@@ -20,6 +20,7 @@ PACK = 4
 QUAD = 32
 GROUP = 16
 HALF = S // 2
+FIRST_WORDS = 256
 
 
 def tile_picked_pinball_none_p_kernel(
@@ -47,13 +48,15 @@ def tile_picked_pinball_none_p_kernel(
         def entries(list_sb, cols):
             return list_sb[:, cols.start // GROUP : cols.stop // GROUP]
 
+        nc.vector.memset(scale_table[:].bitcast(I32), 0)
         nc.vector.memset(e_plane[:].bitcast(I32), 0)
         nc.vector.memset(y_plane[:].bitcast(I32), 0)
-        rows = x_scales[0].bitcast(I32)
-        nc.sync.dma_start(scale_table[:].bitcast(I32), rows.unsqueeze(1).to_broadcast([16, 8, T // 4]))
+        packed = x_words[0].rearrange("p c r -> p (c r)").bitcast(I32)
+        nc.sync.dma_start(word_table[:].bitcast(I32)[:, :FIRST_WORDS], packed[:, :FIRST_WORDS])
         nc.sync.dma_start(obs_sb[:], obs)
+        nc.sync.dma_start(scale_table[:].bitcast(I32)[0:P:8, :], x_scales[0].bitcast(I32))
         nc.sync.dma_start(offs_sb[:], offs)
-        nc.sync.dma_start(word_table[:].bitcast(I32), x_words[0].rearrange("p c r -> p (c r)").bitcast(I32))
+        nc.sync.dma_start(word_table[:].bitcast(I32)[:, FIRST_WORDS:], packed[:, FIRST_WORDS:])
         nc.sync.dma_start(raw_w2[:], w2.rearrange("(p j) c -> p (j c)", j=PACK))
         nc.sync.dma_start(at_sb[:], at)
 

@@ -38,7 +38,6 @@ def tile_picked_pinball_none_p_kernel(
         scale_table = late.tile([P, T], U8, name="scale_table", offset=0, align_bytes=64)
         word_table = keep.tile([P, T], U32, name="word_table", tag="words_then_tau", align_bytes=64)
         e_plane = keep.tile([P, S], U8, name="e_plane", align_bytes=64)
-        y_plane = keep.tile([P, S], U8, name="y_plane", align_bytes=64)
         raw_w2 = keep.tile([P, PACK * N], F32, name="raw_w2")
         tau_rows = tau.rearrange("(v t i) s -> t v i s", t=PACK, i=PACK)
         out_rows = out.rearrange("(v t i) s -> t v i s", t=PACK, i=PACK)
@@ -50,7 +49,6 @@ def tile_picked_pinball_none_p_kernel(
 
         nc.vector.memset(scale_table[:].bitcast(I32), 0)
         nc.vector.memset(e_plane[:].bitcast(I32), 0)
-        nc.vector.memset(y_plane[:].bitcast(I32), 0)
         packed = x_words[0].rearrange("p c r -> p (c r)").bitcast(I32)
         nc.sync.dma_start(word_table[:].bitcast(I32)[:, :FIRST_WORDS], packed[:, :FIRST_WORDS])
         nc.sync.dma_start(obs_sb[:], obs)
@@ -64,8 +62,8 @@ def tile_picked_pinball_none_p_kernel(
         y_picked = keep.tile([P, S], U8, name="y_picked", align_bytes=64)
         e_words = keep.tile([P, S], U32, name="e_words", align_bytes=64)
 
-        def place(plane, picked):
-            for r in range(PACK):
+        def place(plane, picked, first):
+            for r in range(first, PACK):
                 nc.sync.dma_start(plane[:].bitcast(I32)[r:P:QUAD, :], picked[:].bitcast(I32)[8 * r : P : QUAD, :])
 
         def pick_y_words(half, tag):
@@ -74,11 +72,10 @@ def tile_picked_pinball_none_p_kernel(
             return words
 
         nc.vector.tensor_copy(e_picked[:], scale_table[:].indirect(obs_sb[:]))
-        place(e_plane, e_picked)
+        place(e_plane, e_picked, 0)
         nc.vector.tensor_copy(y_picked[:], scale_table[:].indirect(offs_sb[:]))
         raw_w1 = late.tile([P, PACK * N], F32, name="raw_w1", offset=0, align_bytes=64)
         nc.sync.dma_start(raw_w1[:], w1.rearrange("(p j) c -> p (j c)", j=PACK))
-        place(y_plane, y_picked)
         nc.vector.tensor_copy(e_words[:], word_table[:].indirect(obs_sb[:]))
         y_words = [pick_y_words(0, "y_words")]
 
@@ -117,7 +114,10 @@ def tile_picked_pinball_none_p_kernel(
         on_vector, on_scalar = nc.vector.tensor_copy, nc.scalar.copy
         q2 = [quantize("w2_%d" % t, interleave("stage_%d" % t, raw_w2, t, 1, on_vector))[0] for t in range(2)]
         late_w2 = interleave("stage_2", raw_w2, 2, 2, on_scalar)
-        y_words.append(pick_y_words(1, "stage_0"))
+        y_plane = keep.tile([P, S], U8, name="y_plane", tag="stage_0", align_bytes=64)
+        nc.vector.tensor_copy(y_plane[:].bitcast(I32), y_picked[:].bitcast(I32))
+        place(y_plane, y_picked, 1)
+        y_words.append(pick_y_words(1, "stage_1"))
         tau_all = keep.tile([P, PACK * S], F32, name="tau_all", tag="words_then_tau", align_bytes=64)
         tau_sb = [tau_all[:, S * t : S * (t + 1)] for t in range(PACK)]
         for t in range(PACK):
@@ -154,8 +154,8 @@ def tile_picked_pinball_none_p_kernel(
             fetch(target[t], windows[t], cols)
             if n in (2, 4):
                 windows.append(empty_e(t + 1, keep.tile([P, S], F32, name="window", tag="window_%d" % (t - 1))))
-        y = [forecast(t, quantize("w1_%d" % t, interleave("stage_%d" % (t + 1), raw_w1, t, 1, on_vector))[0]) for t in range(3)]
-        late_w1 = interleave("stage_4", raw_w1, 3, 1, on_vector)
+        y = [forecast(t, quantize("w1_%d" % t, interleave("stage_%d" % (t + 2), raw_w1, t, 1, on_vector))[0]) for t in range(3)]
+        late_w1 = interleave("stage_5", raw_w1, 3, 1, on_vector)
         miss = [plain("miss_%d" % t) for t in range(PACK)]
         tilt = [plain("tilt_%d" % t) for t in range(PACK)]
         loss = [plain("loss_%d" % t) for t in range(PACK)]

@@ -21,6 +21,7 @@ QUAD = 32
 GROUP = 16
 HALF = S // 2
 FIRST_WORDS = 256
+SHARE = 96
 
 
 def tile_picked_pinball_none_p_kernel(
@@ -157,8 +158,11 @@ def tile_picked_pinball_none_p_kernel(
         y = [forecast(t, quantize("w1_%d" % t, interleave("stage_%d" % (t + 2), raw_w1, t, 1, on_vector))[0]) for t in range(3)]
         late_w1 = interleave("stage_5", raw_w1, 3, 1, on_vector)
         miss = [plain("miss_%d" % t) for t in range(PACK)]
-        tilt = [plain("tilt_%d" % t) for t in range(PACK)]
         loss = [plain("loss_%d" % t) for t in range(PACK)]
+        tilt = [plain("tilt_%d" % t) for t in range(PACK)]
+
+        def weigh(t, cols, engine):
+            engine.tensor_tensor(tilt[t][:, cols], miss[t][:, cols], tau_sb[t][:, cols], ALU.mult)
 
         def finish(t, cols):
             nc.vector.scalar_tensor_tensor(loss[t][:, cols], miss[t][:, cols], 0.0, tilt[t][:, cols], ALU.max, ALU.subtract)
@@ -172,7 +176,11 @@ def tile_picked_pinball_none_p_kernel(
             if n > 1:
                 finish(*steps[n - 2])
             if n == 3:
-                y.append(forecast(PACK - 1, quantize("w1_3", late_w1, "tilt_0")[0]))
-            nc.vector.tensor_tensor(tilt[t][:, cols], miss[t][:, cols], tau_sb[t][:, cols], ALU.mult)
+                y.append(forecast(PACK - 1, quantize("w1_3", late_w1, "last_codes")[0]))
+            if n < len(steps) - 1:
+                weigh(t, slice(cols.start + SHARE, cols.stop), nc.vector)
+                weigh(t, slice(cols.start, cols.start + SHARE), nc.gpsimd)
+            else:
+                weigh(t, cols, nc.vector)
         for step in steps[-2:]:
             finish(*step)

@@ -171,16 +171,22 @@ def tile_picked_pinball_none_p_kernel(
             elif cols.stop == S:
                 nc.sync.dma_start(out_rows[t], loss[t][:])
 
+        helped = range(1, len(steps) - 1)
+
+        def weigh_rest(n):
+            t, cols = steps[n]
+            weigh(t, slice(cols.start + (SHARE if n in helped else 0), cols.stop), nc.vector)
+
         for n, (t, cols) in enumerate(steps):
             nc.vector.tensor_tensor(miss[t][:, cols], y[t][n % 2], target[t][:, cols], ALU.subtract)
+            if n in helped:
+                weigh(t, slice(cols.start, cols.start + SHARE), nc.gpsimd)
+            if n == 0:
+                y.append(forecast(PACK - 1, quantize("w1_3", late_w1)[0]))
+            if n > 0:
+                weigh_rest(n - 1)
             if n > 1:
                 finish(*steps[n - 2])
-            if n == 3:
-                y.append(forecast(PACK - 1, quantize("w1_3", late_w1, "last_codes")[0]))
-            if n < len(steps) - 1:
-                weigh(t, slice(cols.start + SHARE, cols.stop), nc.vector)
-                weigh(t, slice(cols.start, cols.start + SHARE), nc.gpsimd)
-            else:
-                weigh(t, cols, nc.vector)
+        weigh_rest(len(steps) - 1)
         for step in steps[-2:]:
             finish(*step)

@@ -67,8 +67,7 @@ def tile_picked_pinball_none_p_kernel(
             for r in range(first, PACK):
                 nc.sync.dma_start(plane[:].bitcast(I32)[r:P:QUAD, :], picked[:].bitcast(I32)[8 * r : P : QUAD, :])
 
-        def pick_y_words(half, tag):
-            words = keep.tile([P, HALF], U32, name="y_words", tag=tag, align_bytes=64)
+        def pick_y_words(half, words):
             nc.vector.tensor_copy(words[:], word_table[:].indirect(entries(offs_sb, halves[half])))
             return words
 
@@ -78,10 +77,11 @@ def tile_picked_pinball_none_p_kernel(
         raw_w1 = late.tile([P, PACK * N], F32, name="raw_w1", offset=0, align_bytes=64)
         nc.sync.dma_start(raw_w1[:], w1.rearrange("(p j) c -> p (j c)", j=PACK))
         nc.vector.tensor_copy(e_words[:], word_table[:].indirect(obs_sb[:]))
-        y_words = [pick_y_words(0, "y_words")]
+        y_words = [pick_y_words(0, keep.tile([P, HALF], U32, name="y_words_0", align_bytes=64))]
 
-        def interleave(tag, raw, first, count, copy):
-            grouped = keep.tile([P, count * P * PACK], BF16, name="grouped", tag=tag, align_bytes=64)
+        def interleave(tag, raw, first, count, copy, grouped=None):
+            if grouped is None:
+                grouped = keep.tile([P, count * P * PACK], BF16, name="grouped", tag=tag, align_bytes=64)
             src = raw[:].rearrange("p (j v t i) -> p t v j i", j=PACK, t=PACK, i=PACK)[:, first : first + count]
             copy(grouped[:].rearrange("p (t v i j) -> p t v j i", t=count, i=PACK, j=PACK), src)
             return grouped
@@ -113,12 +113,15 @@ def tile_picked_pinball_none_p_kernel(
             return keep.tile([P, S], F32, name=name, align_bytes=64)
 
         on_vector, on_scalar = nc.vector.tensor_copy, nc.scalar.copy
-        q2 = [quantize("w2_%d" % t, interleave("stage_%d" % t, raw_w2, t, 1, on_vector))[0] for t in range(2)]
+        behind_w1 = 4 * PACK * N
+        first_stage = late.tile([P, P * PACK], BF16, name="first_stage", offset=behind_w1, align_bytes=64)
+        q2 = quantize("w2_0", interleave(None, raw_w2, 0, 1, on_vector, first_stage))
+        q2 = q2 + quantize("w2_1", interleave("stage_1", raw_w2, 1, 1, on_vector))
         late_w2 = interleave("stage_2", raw_w2, 2, 2, on_scalar)
-        y_plane = keep.tile([P, S], U8, name="y_plane", tag="stage_0", align_bytes=64)
+        y_plane = late.tile([P, S], U8, name="y_plane", offset=behind_w1, align_bytes=64)
         nc.vector.tensor_copy(y_plane[:].bitcast(I32), y_picked[:].bitcast(I32))
         place(y_plane, y_picked, 1)
-        y_words.append(pick_y_words(1, "stage_1"))
+        y_words.append(pick_y_words(1, late.tile([P, HALF], U32, name="y_words_1", offset=behind_w1 + S, align_bytes=64)))
         tau_all = keep.tile([P, PACK * S], F32, name="tau_all", tag="words_then_tau", align_bytes=64)
         tau_sb = [tau_all[:, S * t : S * (t + 1)] for t in range(PACK)]
         for t in range(PACK):
@@ -155,7 +158,7 @@ def tile_picked_pinball_none_p_kernel(
             fetch(target[t], windows[t], cols)
             if n in (2, 4):
                 windows.append(empty_e(t + 1, keep.tile([P, S], F32, name="window", tag="window_%d" % (t - 1))))
-        y = [forecast(t, quantize("w1_%d" % t, interleave("stage_%d" % (t + 2), raw_w1, t, 1, on_vector))[0]) for t in range(3)]
+        y = [forecast(t, quantize("w1_%d" % t, interleave("stage_%d" % (3, 2, 4)[t], raw_w1, t, 1, on_vector))[0]) for t in range(3)]
         late_w1 = interleave("stage_5", raw_w1, 3, 1, on_vector)
         miss = [plain("miss_%d" % t) for t in range(PACK)]
         loss = [plain("loss_%d" % t) for t in range(PACK)]

from contextlib import ExitStack

import concourse.mybir as mybir

K, T, S, N = 512, 2048, 512, 512
FLOPS = 2 * 2 * K * N * S

F32 = mybir.dt.float32
BF16 = mybir.dt.bfloat16
I32 = mybir.dt.int32
U32 = mybir.dt.uint32
U16 = mybir.dt.uint16
U8 = mybir.dt.uint8
FP8X4 = mybir.dt.float8_e4m3fn_x4
ALU = mybir.AluOpType
COPY = mybir.ActivationFunctionType.Copy

P = 128
PACK = 4
QUAD = 32
GROUP = 16
HALF = S // 2
FIRST_WORDS = 256
SHARE = 96


def tile_picked_pinball_none_p_kernel(
    tc, x_words, x_scales, w1, w2, tau, offs, obs, at, out
):
    nc = tc.nc
    with ExitStack() as ctx:
        keep = ctx.enter_context(tc.tile_pool(name="keep", bufs=1))
        psum = ctx.enter_context(tc.psum_pool(name="psum", bufs=1))

        late = ctx.enter_context(tc.tile_pool(name="late", bufs=1))
        offs_sb = keep.tile([P, S // GROUP], U16, name="offs_sb")
        obs_sb = keep.tile([P, S // GROUP], U16, name="obs_sb")
        at_sb = keep.tile([P, S // GROUP], U16, name="at_sb")
        scale_table = late.tile([P, T], U8, name="scale_table", offset=0, align_bytes=64)
        word_table = keep.tile([P, T], U32, name="word_table", tag="words_then_tau", align_bytes=64)
        e_plane = keep.tile([P, S], U8, name="e_plane", align_bytes=64)
        raw_w2 = keep.tile([P, PACK * N], F32, name="raw_w2")
        tau_rows = tau.rearrange("(v t i) s -> t v i s", t=PACK, i=PACK)
        out_rows = out.rearrange("(v t i) s -> t v i s", t=PACK, i=PACK)
        whole = slice(0, S)
        halves = [slice(0, HALF), slice(HALF, S)]

        def entries(list_sb, cols):
            return list_sb[:, cols.start // GROUP : cols.stop // GROUP]

        nc.vector.memset(scale_table[:].bitcast(I32), 0)
        nc.vector.memset(e_plane[:].bitcast(I32), 0)
        packed = x_words[0].rearrange("p c r -> p (c r)").bitcast(I32)
        nc.sync.dma_start(word_table[:].bitcast(I32)[:, :FIRST_WORDS], packed[:, :FIRST_WORDS])
        nc.sync.dma_start(obs_sb[:], obs)
        nc.sync.dma_start(scale_table[:].bitcast(I32)[0:P:8, :], x_scales[0].bitcast(I32))
        nc.sync.dma_start(offs_sb[:], offs)
        nc.sync.dma_start(word_table[:].bitcast(I32)[:, FIRST_WORDS:], packed[:, FIRST_WORDS:])
        nc.sync.dma_start(raw_w2[:], w2.rearrange("(p j) c -> p (j c)", j=PACK))
        nc.sync.dma_start(at_sb[:], at)

        e_picked = keep.tile([P, S], U8, name="e_picked", align_bytes=64)
        y_picked = keep.tile([P, S], U8, name="y_picked", align_bytes=64)
        e_words = keep.tile([P, S], U32, name="e_words", align_bytes=64)

        def place(plane, picked, first):
            for r in range(first, PACK):
                nc.sync.dma_start(plane[:].bitcast(I32)[r:P:QUAD, :], picked[:].bitcast(I32)[8 * r : P : QUAD, :])

        def pick_y_words(half, words):
            nc.vector.tensor_copy(words[:], word_table[:].indirect(entries(offs_sb, halves[half])))
            return words

        nc.vector.tensor_copy(e_picked[:], scale_table[:].indirect(obs_sb[:]))
        place(e_plane, e_picked, 0)
        nc.vector.tensor_copy(y_picked[:], scale_table[:].indirect(offs_sb[:]))
        raw_w1 = late.tile([P, PACK * N], F32, name="raw_w1", offset=0, align_bytes=64)
        nc.sync.dma_start(raw_w1[:], w1.rearrange("(p j) c -> p (j c)", j=PACK))
        nc.vector.tensor_copy(e_words[:], word_table[:].indirect(obs_sb[:]))
        y_words = [pick_y_words(0, keep.tile([P, HALF], U32, name="y_words_0", align_bytes=64))]

        def interleave(tag, raw, first, count, copy, grouped=None):
            if grouped is None:
                grouped = keep.tile([P, count * P * PACK], BF16, name="grouped", tag=tag, align_bytes=64)
            src = raw[:].rearrange("p (j v t i) -> p t v j i", j=PACK, t=PACK, i=PACK)[:, first : first + count]
            copy(grouped[:].rearrange("p (t v i j) -> p t v j i", t=count, i=PACK, j=PACK), src)
            return grouped

        def quantize(name, grouped, tag=None):
            width = grouped.shape[1] // PACK
            codes = keep.tile([P, width], U32, name="codes", tag=tag or "codes_" + name, align_bytes=64)
            planes = keep.tile([P, width], U8, name="planes_" + name, align_bytes=64)
            nc.vector.quantize_mx(out=codes[:].bitcast(FP8X4), scales=planes[:], in_=grouped[:])
            return [(codes[:, c : c + P], planes[:, c : c + P]) for c in range(0, width, P)]

        def bank(number, width=S):
            return psum.tile([P, width], F32, name="acc", tag="bank_%d" % number)

        def product(acc, weights, words, scales):
            codes, planes = weights
            nc.tensor.matmul_mx(
                out=acc,
                lhsT=codes.bitcast(FP8X4),
                lhsT_scale=planes,
                rhs=words.bitcast(FP8X4),
                rhs_scale=scales,
                start=True,
                stop=True,
            )
            return acc

        def plain(name):
            return keep.tile([P, S], F32, name=name, align_bytes=64)

        on_vector, on_scalar = nc.vector.tensor_copy, nc.scalar.copy
        behind_w1 = 4 * PACK * N
        first_stage = late.tile([P, P * PACK], BF16, name="first_stage", offset=behind_w1, align_bytes=64)
        q2 = quantize("w2_0", interleave(None, raw_w2, 0, 1, on_vector, first_stage))
        q2 = q2 + quantize("w2_1", interleave("stage_1", raw_w2, 1, 1, on_vector))
        late_w2 = interleave("stage_2", raw_w2, 2, 2, on_scalar)
        y_plane = late.tile([P, S], U8, name="y_plane", offset=behind_w1, align_bytes=64)
        nc.vector.tensor_copy(y_plane[:].bitcast(I32), y_picked[:].bitcast(I32))
        place(y_plane, y_picked, 1)
        y_words.append(pick_y_words(1, late.tile([P, HALF], U32, name="y_words_1", offset=behind_w1 + S, align_bytes=64)))
        tau_all = keep.tile([P, PACK * S], F32, name="tau_all", tag="words_then_tau", align_bytes=64)
        tau_sb = [tau_all[:, S * t : S * (t + 1)] for t in range(PACK)]
        for t in range(PACK):
            nc.sync.dma_start(tau_sb[t], tau_rows[t])
        q2 = q2 + quantize("w2_23", late_w2)

        def empty_e(t, window):
            for number, cols, copy in e_pieces[t]:
                acc = bank(number, cols.stop - cols.start)
                copy(window[:, cols], product(acc[:], q2[t], e_words[:, cols], e_plane[:, cols]))
            return window

        def fetch(picked, window, cols):
            nc.scalar.activation(picked[:, cols], window[:].indirect(entries(at_sb, cols)), COPY)

        def forecast(t, weights):
            if t == 0:
                accs = [bank(number, HALF)[:] for number in (PACK, 0)]
            else:
                acc = bank(PACK + t)
                accs = [acc[:, cols] for cols in halves]
            return [product(accs[half], weights, y_words[half][:], y_plane[:, cols]) for half, cols in enumerate(halves)]

        e_pieces = [
            [(0, halves[0], on_scalar), (7, halves[1], on_scalar)],
            [(1, halves[0], on_scalar), (6, halves[1], on_scalar)],
            [(2, whole, on_scalar)],
            [(3, whole, on_scalar)],
        ]
        steps = [(t, cols) for t in range(PACK) for cols in halves]
        target = [plain("target_%d" % t) for t in range(PACK)]
        windows = [empty_e(t, keep.tile([P, S], F32, name="window", tag="window_%d" % t)) for t in range(2)]
        for n, (t, cols) in enumerate(steps):
            fetch(target[t], windows[t], cols)
            if n in (2, 4):
                windows.append(empty_e(t + 1, keep.tile([P, S], F32, name="window", tag="window_%d" % (t - 1))))
        y = [forecast(t, quantize("w1_%d" % t, interleave("stage_%d" % (3, 2, 4)[t], raw_w1, t, 1, on_vector))[0]) for t in range(3)]
        late_w1 = interleave("stage_5", raw_w1, 3, 1, on_vector)
        miss = [plain("miss_%d" % t) for t in range(PACK)]
        loss = [plain("loss_%d" % t) for t in range(PACK)]
        tilt = [plain("tilt_%d" % t) for t in range(PACK)]

        def weigh(t, cols, engine):
            engine.tensor_tensor(tilt[t][:, cols], miss[t][:, cols], tau_sb[t][:, cols], ALU.mult)

        def finish(t, cols):
            nc.vector.scalar_tensor_tensor(loss[t][:, cols], miss[t][:, cols], 0.0, tilt[t][:, cols], ALU.max, ALU.subtract)
            if t == PACK - 1:
                nc.sync.dma_start(out_rows[t][:, :, cols], loss[t][:, cols])
            elif cols.stop == S:
                nc.sync.dma_start(out_rows[t], loss[t][:])

        helped = range(1, len(steps) - 1)

        def weigh_rest(n):
            t, cols = steps[n]
            weigh(t, slice(cols.start + (SHARE if n in helped else 0), cols.stop), nc.vector)

        for n, (t, cols) in enumerate(steps):
            nc.vector.tensor_tensor(miss[t][:, cols], y[t][n % 2], target[t][:, cols], ALU.subtract)
            if n in helped:
                weigh(t, slice(cols.start, cols.start + SHARE), nc.gpsimd)
            if n == 0:
                y.append(forecast(PACK - 1, quantize("w1_3", late_w1)[0]))
            if n > 0:
                weigh_rest(n - 1)
            if n > 1:
                finish(*steps[n - 2])
        weigh_rest(len(steps) - 1)
        for step in steps[-2:]:
            finish(*step)
